import numpy as np, ml_dtypes
CORES = [1,5,17,21,33,37,49,53]
N = 8
BF = ml_dtypes.bfloat16
S, D, H, CAP = 3072, 4, 32, 2048
def heads(x):
    return x.astype(np.float32).reshape(N, 8, 16, S)
def scores(z, v, t):
    return np.einsum("rgcs,rgc->rgs", z, v[:, :, t].astype(np.float32).reshape(N, 8, 16))
def layer(z, kept, w, gap, t):
    out = z.copy()
    for g in range(8):
        q = np.concatenate([z[r, g][:, kept[r][g]] for r in range(N)], axis=1)
        q = np.pad(q, ((0, 0), (H, H))); a = H
        for r in range(N):
            k = kept[r][g].size; d = int(gap[r, 16 * g, t])
            m = w[r, 16 * g:16 * g + 16, 48 * t:48 * t + 48].astype(np.float32)
            s = m[:, :16].T @ q[:, a:a + k] + m[:, 16:32].T @ q[:, a - d:a - d + k] + m[:, 32:].T @ q[:, a + d:a + d + k]
            out[r, g][:, kept[r][g]] = np.clip(np.rint(s * np.float32(0.125)), -15, 15)
            a += k
    return out
def run(x, v, w, th, gap):
    z = heads(x); kept = [[np.arange(S)] * 8 for r in range(N)]; cnt = np.zeros((D, N, 8), np.int64)
    for t in range(D):
        s = scores(z, v, t)
        kept = [[kept[r][g][s[r, g, kept[r][g]] >= th[r, 16 * g, t]] for g in range(8)] for r in range(N)]
        for r in range(N):
            for g in range(8): cnt[t, r, g] = kept[r][g].size
        z = layer(z, kept, w, gap, t)
    return z, cnt
def rows16(a):
    return np.repeat(a, 16, axis=1).astype(np.int32)
def shares(rng):
    k = [rng.integers(CAP // 2, CAP * 7 // 8 + 1, (N, 8))]
    for t in range(1, D): k.append(np.maximum(k[-1] * rng.integers(60, 91, (N, 8)) // 100, H))
    return np.stack(k)
def settle(d, want):
    x, v, w, gap = d["x"], d["v"], d["w"], d["gap"]
    z = heads(x); kept = [[np.arange(S)] * 8 for r in range(N)]; th = np.zeros((N, 8, D), np.int32)
    for t in range(D):
        s = scores(z, v, t)
        for r in range(N):
            for g in range(8):
                a = s[r, g, kept[r][g]]; e = np.sort(a)[::-1]; lim = int(e[min(int(want[t, r, g]), e.size) - 1])
                if np.count_nonzero(a >= lim) > CAP: lim += 1
                th[r, g, t] = lim; kept[r][g] = kept[r][g][a >= lim]
        z = layer(z, kept, w, gap, t)
    d["th"] = rows16(th); return d
def setup_inputs(rng):
    d = {"x": rng.integers(-15, 16, (N, 128, S)).astype(np.float32).astype(BF), "v": rng.integers(-7, 8, (N, 128, D)).astype(np.float32).astype(BF),
         "w": (2 * rng.integers(0, 2, (N, 128, 48 * D)) - 1).astype(np.float32).astype(BF), "th": None, "gap": rows16(rng.integers(1, H + 1, (N, 8, D)))}
    return settle(d, shares(rng))
def setup_inputs_caps(rng):
    d = setup_inputs(rng); x = d["x"]; s = scores(heads(x), d["v"], 0); g8 = np.arange(8)
    big = (np.arange(N)[:, None] + g8 + rng.integers(0, 2)) % 2 == 0
    for r in range(N):
        for g in range(8):
            k = CAP if big[r, g] else H; u = s[r, g]; o = np.argsort(-u, kind="stable"); late = o[k:]; late = late[u[late] == u[o[k - 1]]]
            b = x[r, 16 * g:16 * g + 16]; b[:, late] = b[:, o[-1:]]
    want = np.stack([np.where(big, CAP, H)] + [np.where(big & (g8 % 4 < 2), CAP, H)] * (D - 1))
    d["gap"] = rows16(rng.choice(np.array([1, H]), (N, 8, D))); return settle(d, want)
def setup_inputs_ends(rng):
    d = setup_inputs(rng); x = d["x"]; s = scores(heads(x), d["v"], 0); k = int(rng.integers(0, 3))
    for r in range(N):
        for g in range(8):
            o = np.argsort(-s[r, g], kind="stable"); m = (r + g + k) % 3
            if m == 1: o = o[::-1]
            if m == 2: o = np.concatenate([o[0::2], o[1::2][::-1]])
            x[r, 16 * g:16 * g + 16] = x[r, 16 * g:16 * g + 16][:, o]
    d["gap"] = rows16(rng.choice(np.array([1, H]), (N, 8, D))); return settle(d, shares(rng))
def setup_inputs_ties(rng):
    d = setup_inputs(rng); c = rng.integers(0, 16, (N, 8, 1, D)); sg = 2 * rng.integers(0, 2, (N, 8, 1, D)) - 1
    d["v"] = ((np.arange(16)[:, None] == c) * sg).reshape(N, 128, D).astype(np.float32).astype(BF)
    return settle(d, shares(rng))
def setup_inputs_spread(rng):
    d = setup_inputs(rng); m = rng.integers(0, 16, (N, 8, 1, S))
    d["x"] = np.rint((2 * rng.random((N, 8, 16, S)) - 1) * m).reshape(N, 128, S).astype(np.float32).astype(BF)
    return settle(d, shares(rng))
def check_inputs(d):
    bad = []; x, v, w = [np.asarray(d[k]).astype(np.float32) for k in ("x", "v", "w")]; th, gap = d["th"], d["gap"]
    if not ((np.rint(x) == x) & (np.abs(x) <= 15)).all(): bad.append("x_whole_within_15")
    if not ((np.rint(v) == v) & (np.abs(v) <= 7)).all(): bad.append("v_whole_within_7")
    if not (np.abs(w) == 1).all(): bad.append("w_one_or_minus_one")
    a = th.reshape(N, 8, 16, D); b = gap.reshape(N, 8, 16, D)
    if (a != a[:, :, :1]).any() or (th < -4096).any() or (th > 4096).any(): bad.append("th")
    if (b != b[:, :, :1]).any() or (gap < 1).any() or (gap > H).any(): bad.append("gap")
    if bad: return bad
    cnt = run(x, v, w, th, gap)[1]
    if cnt.min() < H or cnt.max() > CAP: bad.append("numbers_kept")
    return bad
def reference(x, v, w, th, gap):
    z, cnt = run(x, v, w, th, gap)
    return {"y": z.reshape(N, 128, S).astype(np.float32)}

@@ -1,0 +1,543 @@
+from concourse.bass import DstId, RemoteDMATransfer
+from concourse.mybir import AluOpType as ALU, ActivationFunctionType as ACTF
+
+S, D, CAP, H = 3072, 4, 2048, 32
+MAIN = CAP - H
+BIAS, BIG, CB = 192.0, 65536.0, 4096.0
+DUMP = 2064
+QW = CAP + 3 * H
+CHUNKS = [(32, 512), (544, 512), (1056, 512), (1568, 320), (1888, 128)]
+MERGE_V = 256
+QSPLIT = 1536
+NENG = 8
+FRONT = "s0 s1 k0 n0 c0 a0 s2 u0 w0 k1 m0 c1 b0 n1 d0 m1 a1 u1 p0 b1 w1 d1 p1"
+FIRST = "Vc0 lc f0 h0 Vc1 h1 Ab0 Ab1 f1 r0 Ab2 h2 Ac2 r1 Ab3 e0 f2 gh Ac3 f3 e1 r2 h3 e2 Ab4 Vc4 s0 r3 f4 h4 r4 Ve gr xc e3 e4 gt gg s1"
+MID = "Ab0 Vc0 Ab1 h0 r0 f0 Ac1 h1 Ab2 f1 Vc4 Ac2 e0 r1 f2 gh e1 h3 h2 f3 Vc3 Ab3 s0 f4 Ve r2 gr r3 Ab4 e2 gt e3 h4 r4 e4 gg s1"
+LAST = ("h0 Vc0 f0 Ab0 r0 f1 h1 Ab1 e0 f2 Ac1 r1 gh f3 Ab2 Ae e1 Ac2 gr h2 f4 gg gt r2 Vy0-3 Vc3 h3 Ay3-8 Ab3 h4 e2 r3 Ab4 Vc4 "
+        "r4 e3 Ay8-12 e4 Ay12-18 Vy18-24")
+BF, F32, I32, U16 = "bfloat16", "float32", "int32", "uint16"
+
+SCRATCH = {"ws": ("sbuf", [128, 12, 16], BF), "wd": ("sbuf", [128, 12, 128], BF)}
+for _dt, _bufs in (
+        (BF, dict(xs=S, vs=8, JH=144, JG=128, z=256, za=128, tab=256, hi=384, wt=384, vt=576, bcode=144, bcm=144, bcs=144,
+                  bd=152, dm=14 * 128, G=128, L0=128, L1=128, BI=128, cb=128, ones=512, mk0=200, cs0=200, mkf=136, csf=136,
+                  val=136, ab=576, csb=200, tb=CAP, tc=CAP, eb=64, ec=64)),
+        (F32, dict(yo=S, J=384, col=32, pw0=8, pw=8, rv=16, gm=8, nt=192, dt_=24, cv=132, tp=36, thf=4, thb=4, gf=4, gf2=4,
+                   vf=4, ta=24, tb_=24, cc=8, f1=192, f2=192)),
+        (I32, dict(thi=4, gpi=4, pi=4, pa=4)),
+        (U16, dict(lm=160, lp=160, cu=24, du=24, ix=128, fu=192))):
+    for _n, _w in _bufs.items():
+        SCRATCH[_n] = ("sbuf", [128, _w], _dt)
+for _t in range(D):
+    SCRATCH["yz%d" % _t] = ("sbuf", [128, S + CAP + H], BF)
+    SCRATCH["qb%d" % _t] = ("sbuf", [128, QW], BF)
+    SCRATCH["m%d" % _t] = ("sbuf", [128, 16 + DUMP + 384], BF)
+for _b in range(8):
+    SCRATCH["b%d" % _b] = ("psum", [128, 512], F32)
+
+NDMA = 8
+SEMAPHORES = ["sV", "sA", "sP", "sG", "sent", "ys"] + ["arr%d" % t for t in range(D)] + ["d%d" % i for i in range(NDMA)]
+
+
+def build(g, core, T, topo, rank):
+    ops = []
+    V, A, P = g.vector, g.scalar, g.tensor
+
+    def op(eng, fn, rd, wr, sem=None, val=None):
+        ops.append({"e": eng, "fn": fn, "rd": rd, "wr": wr, "sem": sem, "val": val})
+
+    def ap(n, a, b, step=1):
+        return T[n][:, a:b:step] if step != 1 else T[n][:, a:b]
+
+    def sc(x):
+        return (ap(x[0], x[1], x[1] + 1), [(x[0], x[1], x[1] + 1)]) if isinstance(x, tuple) else (x, [])
+
+    def src(i, lst):
+        if lst is None:
+            return ap(*i), [i[:3]]
+        return ap(*i).indirect(ap(*lst)), [i[:3], lst]
+
+    def ts(o, i, s1, o0, s2=None, o1=None, lst=None):
+        a1, r1 = sc(s1)
+        a2, r2 = sc(s2)
+        x, r = src(i, lst)
+        if o1 is None:
+            op("V", lambda: V.tensor_scalar(ap(*o), x, a1, None, o0), r + r1, [o])
+        else:
+            op("V", lambda: V.tensor_scalar(ap(*o), x, a1, a2, o0, o1), r + r1 + r2, [o])
+
+    def tt(o, i0, i1, o0, lst=None):
+        x, r = src(i0, lst)
+        op("V", lambda: V.tensor_tensor(ap(*o), x, ap(*i1), o0), r + [i1], [o])
+
+    def cp(o, i, lst=None):
+        x, r = src(i, lst)
+        op("V", lambda: V.tensor_copy(ap(*o), x), r, [o])
+
+    def ms(o, c):
+        op("V", lambda: V.memset(ap(*o), c), [], [o])
+
+    def scan(o, i, first=0.0, op0=ALU.add, op1=ALU.max):
+        a1, r1 = sc(first)
+        op("V", lambda: V.tensor_tensor_scan(ap(*o), ap(*i), ap(*i), a1, op0, op1), [i] + r1, [o])
+
+    def act(o, i, scale=1.0, bias=0.0, lst=None):
+        a1, r1 = sc(scale)
+        a2, r2 = sc(bias)
+        x, r = src(i, lst)
+        op("A", lambda: A.activation(ap(*o), x, ACTF.Identity, bias=a2, scale=a1), r + r1 + r2, [o])
+
+    def gat(eng, o, win, lst, scale=1.0, bias=0.0):
+        if eng == "A":
+            act(o, win, scale, bias, lst)
+        elif scale == 1.0 and bias == 0.0:
+            cp(o, win, lst)
+        else:
+            ts(o, win, scale, ALU.mult, bias, ALU.add, lst)
+
+    def mm(o, l, r, start, stop):
+        lap = T.wd[:, l[1], :] if l[0] == "wd" else ap(*l)
+        lr = ("wd", 0, 128) if l[0] == "wd" else l
+        op("P", lambda: P.matmul(ap(*o), lap, ap(*r), start, stop), [lr, r[:3]], [o])
+
+    def iota(o, pat, base=0, mult=0):
+        if o[0] == "pi":
+            op("G", lambda: g.iota(ap(*o), pat, base, mult), [], [o])
+        else:
+            op("G", lambda: g.iota(ap(*o), pat, base, mult, allow_small_or_imprecise_dtypes=True), [], [o])
+
+    def asel(o, i, cmp, fill):
+        op("G", lambda: g.affine_select(ap(*o), ap(*i), [[1, 128]], cmp, fill, 0, -1), [i], [o])
+
+    nd = [0]
+
+    def load(eng, o, dst, s):
+        q = g.sync if eng == "S" else A
+        op(eng, lambda: q.dma_start(dst, s), [], [o], "d%d" % nd[0], 16)
+        nd[0] += 1
+
+    load("A", ("vs", 0, 4), T.vs[:, 0:4], T.v[:])
+    load("A", ("thi", 0, 4), T.thi[:], T.th[:])
+    for j in range(3):
+        load("S", ("xs", 1024 * j, 1024 * j + 1024), T.xs[:, 1024 * j:1024 * j + 1024], T.x[:, 1024 * j:1024 * j + 1024])
+    load("S", ("ws", 0, 16), T.ws[:], T.w[:])
+    load("S", ("gpi", 0, 4), T.gpi[:], T.gap[:])
+
+    G16, R, R8, HH, CA, CE, CD, WR, LO, TC_, HA, HB, CH, GG = range(14)
+    iota(("pi", 0, 1), [[0, 1]], 0, 1)
+    iota(("J", 0, 384), [[1, 384]])
+    iota(("JH", 0, 144), [[1, 72], [0, 2]])
+    iota(("JG", 0, 128), [[1, 8], [0, 16]])
+    iota(("m0", 0, DUMP), [[0, DUMP]])
+    iota(("ones", 0, 512), [[0, 512]], 1)
+    ms(("mk0", 192, 200), 0.0)
+    ms(("cs0", 0, 1), 0.0)
+    for j, bits in enumerate((112, 15, 7)):
+        ts(("pa", j, j + 1), ("pi", 0, 1), bits, ALU.bitwise_and)
+    cp(("col", 0, 3), ("pa", 0, 3))
+
+    def table():
+        ts(("z", 0, 1), ("col", R8, R8 + 1), 8.0, ALU.mult)
+        yield
+        for i in range(8):
+            n = 1 << i
+            ts(("za", 0, n), ("z", 0, n), -8.0, ALU.add, float(i - 8), ALU.max)
+            yield
+            tt(("z", n, 2 * n), ("z", 0, n), ("za", 0, n), ALU.min)
+            yield
+        ts(("tab", 0, 256), ("z", 0, 256), 0.0, ALU.min, ("col", TC_), ALU.max)
+        yield
+
+    def c1(j, i, s1, o0, s2=None, o1=None):
+        ts(("col", j, j + 1), ("col", i, i + 1), s1, o0, s2, o1)
+
+    def c2(j, i, scale, bias):
+        act(("col", j, j + 1), ("col", i, i + 1), scale, bias)
+
+    def onehot(o, i, c, w=None):
+        if w is None:
+            ts(o, i, ("col", c), ALU.is_equal)
+        else:
+            ts(o, i, ("col", c), ALU.is_equal, w, ALU.mult)
+
+    def vtile(t):
+        onehot(("vt", 144 * t, 144 * t + 144), ("J", 0, 144), CE, ("vf", t))
+
+    def lists(t):
+        ts(("lm", 40 * t + 4, 40 * t + 36), ("tp", 0, 32), ("gf", t), ALU.subtract)
+        ts(("lp", 40 * t, 40 * t + 36), ("tp", 0, 36), ("gf", t), ALU.add)
+
+    def first_columns():
+        c1(HH, R, 8.0, ALU.is_ge)
+        for j, i, scale, bias in ((WR, HH, 7.0, 1.0), (GG, G16, 0.0625, 0.0), (LO, HH, -1.0, 1.0), (CH, G16, 0.5, 7.0),
+                                  (TC_, HH, 7.0, -8.0), (HA, HH, -1.0, 0.0), (HB, HH, 190.0, 1.0)):
+            c2(j, i, scale, bias)
+
+    early = [
+        first_columns,
+        lambda: c1(CE, G16, 15.0, ALU.add),
+        lambda: c1(CA, HH, ("col", G16), ALU.add, 14.0, ALU.add),
+        lambda: c1(CD, R8, ("col", CE), ALU.add),
+        lambda: ts(("pw0", 0, 8), ("J", 0, 8), ("col", R8), ALU.is_lt, 1.0, ALU.add),
+        lambda: ts(("rv", 0, 7), ("J", 1, 8), ("col", R8), ALU.is_le),
+        lambda: ts(("rv", 7, 14), ("J", 0, 7), ("col", R8), ALU.is_ge),
+        lambda: onehot(("bd", 0, 152), ("J", 0, 152), CD, ("col", WR)),
+        lambda: scan(("pw", 0, 8), ("pw0", 0, 8), -CB, ALU.mult, ALU.min),
+        lambda: onehot(("gm", 0, 8), ("J", 0, 8), GG),
+        lambda: cp(("vf", 0, 4), ("vs", 0, 4)),
+        lambda: onehot(("bcode", 0, 144), ("J", 0, 144), CA, ("pw", 7)),
+        lambda: vtile(0),
+        lambda: onehot(("bcm", 0, 144), ("J", 0, 144), CE, ("col", LO)),
+        lambda: onehot(("bcs", 0, 144), ("JH", 0, 144), CH),
+        lambda: cp(("thf", 0, 4), ("thi", 0, 4)),
+        lambda: onehot(("G", 0, 128), ("JG", 0, 128), GG),
+    ]
+    steps = table()
+    for j in range(18):
+        if j < len(early):
+            early[j]()
+        next(steps)
+    asel(("L0", 0, 128), ("G", 0, 128), ALU.is_gt, 0.0)
+    asel(("L1", 0, 128), ("L0", 0, 128), ALU.not_equal, float(S))
+    asel(("BI", 0, 128), ("L0", 0, 128), ALU.not_equal, BIG)
+    asel(("BI", 0, 128), ("BI", 0, 128), ALU.is_equal, 0.0)
+    act(("nt", 0, 192), ("J", 0, 192), 16.0, ("col", R))
+    act(("hi", 0, 384), ("J", 0, 384), ("col", HA), ("col", HB))
+    act(("dt_", 0, 24), ("nt", 0, 24), 1.0, float(DUMP))
+    diag = {}
+    for dl in range(-7, 16):
+        base = ("bd", 15 - dl, 143 - dl)
+        if 0 <= dl <= 8:
+            diag[dl] = base
+        else:
+            j = -dl - 1 if dl < 0 else 22 - dl
+            diag[dl] = ("dm", 128 * j, 128 * j + 128)
+            act(diag[dl], base, ("rv", j))
+
+    def weights():
+        for q in range(8):
+            op("A", lambda q=q: A.activation(T.wd[:, :, 16 * q:16 * q + 16], T.ws[:], ACTF.Identity, scale=T.gm[:, q:q + 1]),
+               [("ws", 0, 16), ("gm", q, q + 1)], [("wd", 16 * q, 16 * q + 16)])
+
+    def xcopy(n0=2048, n1=S):
+        act(("yz0", n0, n1), ("xs", n0, n1), 1.0, BIAS)
+
+    def later_a():
+        cp(("gf", 0, 4), ("gpi", 0, 4))
+        act(("cb", 0, 128), ("ones", 0, 128), BIAS / 128)
+        act(("gf2", 0, 4), ("gf", 0, 4), 1.0, float(S - H))
+
+    def later_b():
+        act(("tp", 0, 32), ("nt", 0, 32), 1.0, 32.0)
+        act(("tp", 32, 34), ("nt", 0, 2), 1.0, float(H + CAP))
+        act(("tp", 34, 36), ("nt", 0, 2), 1.0, 32.0)
+        act(("cv", 0, 126), ("nt", 0, 126), 1.0, float(S))
+        act(("cv", 126, 128), ("nt", 0, 2), 0.0, -1.0)
+        act(("cv", 128, 130), ("nt", 0, 2), 1.0, float(S))
+        for t in range(D):
+            if rank == 0:
+                iota(("qb%d" % t, 0, H), [[0, H]])
+            if rank == len(T.cores) - 1:
+                iota(("qb%d" % t, QW - H, QW), [[0, H]])
+        iota(("mkf", 128, 136), [[0, 8]])
+        iota(("csf", 0, 1), [[0, 1]])
+        iota(("csb", 0, 1), [[0, 1]])
+
+    def later_c():
+        mm(("b5", 0, 4), ("G", 0, 128), ("vs", 0, 4), True, True)
+        ts(("thb", 0, 4), ("b5", 0, 4), BIAS, ALU.mult, BIG, ALU.add)
+        vtile(1)
+        tt(("thb", 0, 4), ("thb", 0, 4), ("thf", 0, 4), ALU.add)
+
+    def yoff(t):
+        return H if t == D - 1 else 0
+
+    def zoff(t):
+        return S + yoff(t)
+
+    def scores(bank, t, buf, c0, k0, k1, alive):
+        o = (bank, k0, k1)
+        if alive is not None:
+            mm(o, ("BI", 0, 128), (alive[0], alive[1] + k0, alive[1] + k1), True, False)
+        for r in range(16):
+            mm(o, ("vt", 144 * t + 15 - r, 144 * t + 143 - r), (buf, c0 + 16 * k0 + r, c0 + 16 * k1, 16),
+               alive is None and r == 0, r == 15)
+
+    def merge(eng, t, n0, n1):
+        gat(eng, ("yz%d" % t, yoff(t) + n0, yoff(t) + n1), ("yz%d" % (t - 1), 0, S + CAP), ("fu", n0 // 16, n1 // 16))
+
+    def out(eng, n0, n1):
+        gat(eng, ("yo", n0, n1), ("yz%d" % (D - 1), 0, zoff(D - 1) + min(n1, MAIN)), ("fu", n0 // 16, n1 // 16), 1.0, -BIAS)
+        op("S", lambda: g.sync.dma_start(T.y[:, n0:n1], T.yo[:, n0:n1]), [("yo", n0, n1)], [], "ys", 16)
+
+    def send(t):
+        qb = "qb%d" % t
+        left, right = (qb, 0, H), (qb, QW - H, QW)
+        peers = []
+        if rank > 0:
+            peers.append((T.cores[rank - 1], (qb, H, 2 * H), right, left))
+        if rank < len(T.cores) - 1:
+            peers.append((T.cores[rank + 1], (qb, H + CAP, 2 * H + CAP), left, right))
+        peers.sort(key=lambda p: len(topo.engines(core, p[0])))
+        used, tr = [], []
+        for dst, s, d, _ in peers:
+            e = [x for x in topo.engines(core, dst) if x not in used][:NENG]
+            used += e
+            rid, pid = topo.addr(dst)[:2]
+            tr.append(RemoteDMATransfer(dst_ids=[DstId(rid=rid, pnc=pid)], dma_engine_mask=sum(1 << x for x in e),
+                                        remote_sem=T.sem["arr%d" % t], src=ap(*s), dst=ap(*d)))
+        op("G", lambda: g.remote_dma_fused(tr, local_sem=T.sem.sent), [p[1] for p in peers], [], "sent", NENG * len(peers))
+        op(None, None, [], [p[3] for p in peers], "arr%d" % t, NENG * len(peers))
+
+    def keep(t, o, i):
+        ts(o, i, ("thf", 0) if t == 0 else ("thb", t), ALU.is_ge)
+
+    for t in range(D):
+        K = (S if t == 0 else CAP) // 16
+        KU = K // 8
+        mk, cs = ("mk0", "cs0") if t == 0 else ("mkf", "csf")
+        qb, m, yz = "qb%d" % t, "m%d" % t, "yz%d" % t
+        lm, lp = 40 * t, 40 * t
+        cA, cB = ("cc", 2 * t), ("cc", 2 * t + 1)
+        last = t == D - 1
+
+        def step(w, k0, k1, bc, bp, mk=mk, cs=cs, m=m, K=K):
+            a, b = k0 // 8, k1 // 8
+            e = 8 if k1 == K else 0
+            if w == "c":
+                for q in range(8):
+                    mm((bc, a, b), ("bcode", 14 - 2 * q, 142 - 2 * q), (mk, k0 + q, k1, 8), q == 0, q == 7)
+            if w == "n":
+                scan((cs, k0 + 1, k1 + max(e, 1)), (mk, k0, k1 + max(e, 1) - 1), (cs, k0) if k0 else 0.0)
+            if w == "m":
+                o = (bp, a, (k1 + e) // 8)
+                for q in range(8):
+                    mm(o, ("bcm", 14 - 2 * q, 142 - 2 * q), (mk, k0 + q, k1 + e, 8), q == 0, False)
+                for q in range(8):
+                    mm(o, ("bcs", 14 - 2 * q, 142 - 2 * q), (cs, k0 + q, k1 + e, 8), False, q == 7)
+            if w == "u":
+                ts(("cu", a, b), (bc, a, b), -1.0 / CB, ALU.mult)
+            if w == "a":
+                tt(("ta", a, b), (bc, a, b), ("dt_", a, b), ALU.add)
+            if w == "w":
+                tt(("wt", 16 * a, 16 * b), ("tab", 0, 256), ("hi", 16 * a, 16 * b), ALU.mult, ("cu", a, b))
+            if w == "b":
+                tt(("tb_", a, b), (bp, a, b), ("ta", a, b), ALU.max)
+            if w == "d":
+                cp(("du", a, b), ("tb_", a, b))
+            if w == "p":
+                wn = (m, 16, 16 + DUMP + 384)
+                op("V", lambda: V.tensor_copy(ap(*wn).indirect(ap("du", a, b)), ap("wt", 16 * a, 16 * b)),
+                   [("wt", 16 * a, 16 * b), ("du", a, b)], [wn])
+
+        if t == 0:
+            parts = [(0, 128, "b0", "b1"), (128, K, "b5", "b6")]
+            later_b()
+            xcopy(0, 2048)
+            weights()
+            for w in FRONT.split():
+                j = int(w[1])
+                if w[0] == "s":
+                    scores("b7" if j == 2 else "b4", 0, "xs", 0, 64 * j, 64 * j + 64, None)
+                elif w[0] == "k":
+                    keep(0, (mk,) + parts[j][:2], (("b4", "b7")[j],) + parts[j][:2])
+                else:
+                    step(w[0], *parts[j])
+        else:
+            merge("A", t, 0, S - MERGE_V)
+            keep(t, (mk, 2, 66), ("b4", 2, 66))
+            lists(t)
+            if not last:
+                vtile(t + 1)
+            keep(t, (mk, 66, 128), ("b7", 66, 128))
+            keep(t, (mk, 0, 2), ("b7", 128, 130))
+            for w in "cnmuawbdp":
+                step(w, 0, K, "b5", "b6")
+                if w == "m":
+                    for j in range(3):
+                        mm(("b%d" % j, 0, CHUNKS[j][1]), ("cb", 0, 128), ("ones", 0, CHUNKS[j][1]), True, False)
+        for h, bank in enumerate(("b7", "b3")):
+            for dl in range(-7, 16):
+                c0 = 16 + dl + 1024 * h
+                mm((bank, 0, 64), diag[dl], (m, c0, c0 + 1009, 16), dl == -7, dl == 15)
+        if t == 0:
+            later_a()
+            lists(0)
+        ts(cA + (cA[1] + 1,), ("b6", KU, KU + 1), float(S - H), ALU.add)
+        ts(cB + (cB[1] + 1,), ("b6", KU, KU + 1), -1.0, ALU.mult, float(-S if last else CAP), ALU.add)
+        ts(("lm", lm, lm + 2), ("nt", 0, 2), cA, ALU.add, float(-S), ALU.add)
+        ts(("lm", lm + 2, lm + 4), ("nt", 0, 2), cA, ALU.add, ("gf2", t), ALU.subtract)
+        if not last:
+            ts(("val", 0, 130), ("cv", 0, 130), cA, ALU.is_lt)
+        if t > 0 and MERGE_V:
+            merge("V", t, S - MERGE_V, S)
+        win = ("xs", 0, S) if t == 0 else ("yz%d" % (t - 1), S, S + CAP)
+        qbias = 0.0 if t == 0 else -BIAS / 8
+
+        def qg(eng, c0, c1_):
+            gat(eng, (qb, H + c0, H + c1_), win, ("ix", c0 // 16, c1_ // 16), 0.125, qbias)
+
+        ts(("ix", 0, 64), ("b7", 0, 64), 1536.0, ALU.add)
+        qg("A", 0, 512)
+        qg("V", 512, 1024)
+        ts(("ix", 64, 128), ("b3", 0, 64), 1536.0, ALU.add)
+        qg("A", 1024, QSPLIT)
+        qg("V", QSPLIT, CAP)
+        gat("V", (qb, H + CAP, 2 * H + CAP), (qb, H, H + CAP), ("lm", lm, lm + 2))
+        send(t)
+        if not last:
+            iota(("m%d" % (t + 1), 0, DUMP), [[0, DUMP]])
+        if t > 0:
+            al = ("ab", 192 * (t - 1))
+            scores("b5", t, yz, yoff(t), 0, 192, ("mk0", 0) if t == 1 else ("ab", 192 * (t - 2)))
+        else:
+            al = ("mk0", 0)
+
+        def tap(eng, which, j):
+            c0, n = CHUNKS[j]
+            lst = ("lm", lm + 4, lm + 4 + n // 16) if which == "tb" else ("lp", lp, lp + n // 16)
+            gat(eng, (which, c0, c0 + n), (qb, c0, c0 + n + 2 * H), lst)
+
+        def head(j):
+            c0, n = CHUNKS[j]
+            o = ("b%d" % (j % 3), 0, n)
+            if j >= 3 or t == 0:
+                mm(o, ("cb", 0, 128), ("ones", 0, n), True, False)
+            mm(o, ("wd", 3 * t), (qb, H + c0, H + c0 + n), False, False)
+
+        def rest(j):
+            c0, n = CHUNKS[j]
+            o = ("b%d" % (j % 3), 0, n)
+            mm(o, ("wd", 3 * t + 1), ("tb", c0, c0 + n), False, False)
+            mm(o, ("wd", 3 * t + 2), ("tc", c0, c0 + n), False, True)
+
+        def clip(o, i):
+            ts(o, i, BIAS - 15, ALU.max, BIAS + 15, ALU.min)
+
+        def evac(j):
+            c0, n = CHUNKS[j]
+            clip((yz, zoff(t) + c0, zoff(t) + c0 + n), ("b%d" % (j % 3), 0, n))
+
+        def fwd(j):
+            a = (al[0], al[1], al[1] + 192)
+            if j == 0 and t > 0:
+                keep(t, a, ("b5", 0, 192))
+            if j == 1:
+                if t > 0:
+                    scan(("csb", 1, 193), a)
+                mm(("b6", 0, 192), ("L1", 0, 128), a, True, False)
+                mm(("b6", 0, 192), ("G", 0, 128), ("cs0" if t == 0 else "csb", 0, 192), False, True)
+            if j == 2:
+                ts(("f1", 0, 192), ("b6", 0, 192), cA, ALU.is_ge, cB, ALU.mult)
+                tt(("b6", 192, 384), ("b6", 0, 192), ("nt", 0, 192), ALU.max)
+            if j == 3:
+                tt(("f2", 0, 192), ("b6", 192, 384), ("f1", 0, 192), ALU.add)
+            if j == 4:
+                ts(("fu", 0, 192), ("f2", 0, 192), float(yoff(t)), ALU.add)
+
+        def edge_g(eng):
+            gat(eng, ("eb", 0, 64), (qb, 0, H + CAP), ("lm", lm + 2, lm + 6))
+            gat(eng, ("ec", 0, 64), (qb, 0, QW), ("lp", lp + 32, lp + 36))
+
+        def edge_h():
+            mm(("b3", 0, 64), ("cb", 0, 128), ("ones", 0, 64), True, False)
+            mm(("b3", 0, 32), ("wd", 3 * t), (qb, H + CAP, 2 * H + CAP), False, False)
+            mm(("b3", 32, 64), ("wd", 3 * t), (qb, H, 2 * H), False, False)
+
+        def edge_r():
+            mm(("b3", 0, 64), ("wd", 3 * t + 1), ("eb", 0, 64), False, False)
+            mm(("b3", 0, 64), ("wd", 3 * t + 2), ("ec", 0, 64), False, True)
+
+        def edge_tail():
+            if last:
+                clip((yz, 0, H), ("b3", 0, 32))
+            else:
+                clip((yz, S + MAIN, S + CAP + H), ("b3", 0, 64))
+
+        def edge_head():
+            clip((yz, zoff(t), zoff(t) + H), ("b3", 32, 64))
+
+        for w in (LAST if last else FIRST if t == 0 else MID).split():
+            if w[1] in "bc" and w[0] in "AV":
+                tap(w[0], "t" + w[1], int(w[2]))
+            elif w[1] == "e":
+                edge_g(w[0])
+            elif w[1] == "y":
+                out(w[0], *(128 * int(x) for x in w[2:].split("-")))
+            elif w[0] in "href":
+                {"h": head, "r": rest, "e": evac, "f": fwd}[w[0]](int(w[1]))
+            elif w[0] == "s":
+                k0 = 2 + 64 * int(w[1])
+                scores("b7" if int(w[1]) else "b4", t + 1, yz, S, k0, k0 + 64, ("val", 0))
+            else:
+                {"gh": edge_h, "gr": edge_r, "gt": edge_tail, "gg": edge_head, "lc": later_c, "xc": xcopy}[w]()
+    return ops
+
+
+def emit(g, T, ops):
+    queue = {"V": g.vector, "A": g.scalar, "P": g.tensor, "G": g, "S": g.sync}
+    seen = {}
+    for i, o in enumerate(ops):
+        dep = set()
+        acc = [(r, False) for r in o["rd"]] + [(r, True) for r in o["wr"]]
+        for (n, a, b), w in acc:
+            psum = SCRATCH[n][0] == "psum"
+            for j, a2, b2, w2 in seen.get(n, []):
+                e2 = ops[j]["e"]
+                if e2 == o["e"] == "P":
+                    continue
+                if (psum and e2 != o["e"]) or ((w or w2) and a < b2 and a2 < b):
+                    dep.add(j)
+        for (n, a, b), w in acc:
+            seen.setdefault(n, []).append((i, a, b, w))
+        lastof = {}
+        for j in dep:
+            k = ops[j]["e"] if ops[j]["sem"] is None else ("x", j)
+            lastof[k] = max(lastof.get(k, -1), j)
+        o["dep"] = sorted(lastof.values())
+    known = {e: {} for e in queue}
+    for i, o in enumerate(ops):
+        if o["e"] is None:
+            o["clock"], o["wait"] = {}, []
+            continue
+        kn = known[o["e"]]
+        wait = []
+        for j in sorted(o["dep"], reverse=True):
+            p = ops[j]
+            k = p["e"] if p["sem"] is None else ("x", j)
+            if kn.get(k, -1) >= j:
+                continue
+            wait.append(j)
+            kn[k] = j
+            for k2, v in p["clock"].items():
+                kn[k2] = max(kn.get(k2, -1), v)
+        o["wait"] = wait
+        o["clock"] = dict(kn)
+    needed = set(j for o in ops for j in o["wait"])
+    count = {}
+    for i, o in enumerate(ops):
+        if o["sem"] is None and i in needed:
+            o["sem"], o["val"] = "s" + o["e"], 1
+        if o["sem"] is not None:
+            count[o["sem"]] = count.get(o["sem"], 0) + o["val"]
+            o["at"] = count[o["sem"]]
+    waited = {}
+    for o in ops:
+        if o["e"] is None:
+            continue
+        for j in o["wait"]:
+            queue[o["e"]].wait_ge(T.sem[ops[j]["sem"]], ops[j]["at"])
+            waited[ops[j]["sem"]] = max(waited.get(ops[j]["sem"], 0), ops[j]["at"])
+        ins = o["fn"]()
+        if o["sem"] is not None and o["sem"] != "sent":
+            ins.then_inc(T.sem[o["sem"]], o["val"])
+    for s, n in count.items():
+        if waited.get(s, 0) < n:
+            (g.sync if s == "ys" else g).wait_ge(T.sem[s], n)
+
+
+def rank_program(g, core, T, topo):
+    rank = T.rank_of(core)
+    if rank is None:
+        return
+    emit(g, T, build(g, core, T, topo, rank))

@@ -1,37 +1,73 @@
+import math
 from concourse.bass import DstId, RemoteDMATransfer
 from concourse.mybir import AluOpType as ALU, ActivationFunctionType as ACTF
 
 S, D, CAP, H = 3072, 4, 2048, 32
 MAIN = CAP - H
-BIAS, BIG, CB = 192.0, 65536.0, 4096.0
-DUMP = 2064
+ZO = [S + H + (CAP + H) * t for t in range(D)]
+BIAS, ROUND = 192.0, 12582912.0
+TAIL = 2080
+DUMP = 2112
+MW = 16 + DUMP + 512 + CAP
 QW = CAP + 3 * H
-CHUNKS = [(32, 512), (544, 512), (1056, 512), (1568, 320), (1888, 128)]
-MERGE_V = 256
-QSPLIT = 1536
+LW = 72
+CHUNKS = [(32, 480), (512, 512), (1024, 512), (1536, 384), (1920, 96)]
+BANKS = ["b0", "b1", "b2", "b6", "b0"]
+ROWS = [(1, 2, 3), (4, 5, 6, 7), (8, 9, 10, 11), (12, 13, 14), (0,), (15,)]
+LOADS = [0, 1024, 2048, 3072]
+PARTS0 = [(0, 64), (1024, 64), (2048, 64)]
+PARTS = [(0, 128)]
+QCUT = [0, 32, 544, 1024, 1568, 2048]
+YCUT = [0, 512, 1024, 1536, 1920, 2304, 2688, 3072]
+STORES = [0, 512, 1024, 1536, 2304, 3072]
 NENG = 8
-FRONT = "s0 s1 k0 n0 c0 a0 s2 u0 w0 k1 m0 c1 b0 n1 d0 m1 a1 u1 p0 b1 w1 d1 p1"
-FIRST = "Vc0 lc f0 h0 Vc1 h1 Ab0 Ab1 f1 r0 Ab2 h2 Ac2 r1 Ab3 e0 f2 gh Ac3 f3 e1 r2 h3 e2 Ab4 Vc4 s0 r3 f4 h4 r4 Ve gr xc e3 e4 gt gg s1"
-MID = "Ab0 Vc0 Ab1 h0 r0 f0 Ac1 h1 Ab2 f1 Vc4 Ac2 e0 r1 f2 gh e1 h3 h2 f3 Vc3 Ab3 s0 f4 Ve r2 gr r3 Ab4 e2 gt e3 h4 r4 e4 gg s1"
-LAST = ("h0 Vc0 f0 Ab0 r0 f1 h1 Ab1 e0 f2 Ac1 r1 gh f3 Ab2 Ae e1 Ac2 gr h2 f4 gg gt r2 Vy0-3 Vc3 h3 Ay3-8 Ab3 h4 e2 r3 Ab4 Vc4 "
-        "r4 e3 Ay8-12 e4 Ay12-18 Vy18-24")
+ON_VECTOR = [s.split() for s in ("M b0 b1 b3 ec q0 q2 q3 q4 tl", "O0 O1 Q R b2 c0 c1 c3 c4 q0 q1 tl", "O0 O1 Q R c0 c1 c3 q0 q2 q4",
+                                 "O0 O1 R b4 c2 c4 eb q2 q3 q4 tl y1 y3 y6")]
+PUSH = {}
+ORDER = """
+vg.1 tg.1 tg.2 pa.1 ones.1 cb.1 pa.3 pa.2 xs.1 pa.4 col.1 col.8 m0.1 z.1 col.2 pat.1 col.3 col.7 J.1 b0.1 I.1 JG.1 pm.1 col.4
+nt.1 col.5 DI.1 ET.1 xs.2 b2.1 hi0.3 z.2 cs.1 rv.1 Sm.1 bd.1 z.3 m0.2 z.4 hi0.1 col.6 GT.1 rv.2 vf.1 dm.6 b2.2 b4.1 z.5 tf.1
+E.1 hi0.2 col.10 yz.1 csb.1 dm.8 z.6 G.1 b1.1 L0.1 NI.1 vt.1 thf.1 z.7 c44.1 vb.1 b1.2 dm.10 b5.1 dm.12 dm.13 hi0.4 dm.4 m0.4
+z.8 m0.3 zx.2 dm.1 hi.1 L1.2 dm.9 zx.1 b3.1 dm.7 dm.11 b7.1 gm.1 mk.1 cs.2 cd.1 yz.3 gp.1 tab.1 dm.3 b6.1 cu.1 mk.2 L1.1 b6.2
+b6.3 t1.1 b3.2 cd.2 mw.1 wrd.1 nt.2 gn.1 cv.1 dm.2 LN.1 L1.3 b4.2 wt.1 cs.3 xs.3 du.1 dm.14 cu.2 b5.2 lf.2 b6.4 t1.2 m0.5
+mk.3 b4.3 wt.2 lf.1 dm.5 cd.3 du.2 cs.4 col.11 ws.1 wd.3 wd.8 lf.3 b6.5 b6.6 wd.5 hi0.5 vt.2 col.9 wd.6 cu.3 m0.6 col.13 I8.1
+wd.7 L1.4 t1.3 lf.4 lf.9 wt.3 du.3 m0.7 ls.5 b5.3 cv.2 wd.4 m0.8 b7.2 thb.1 ix.1 ls.1 qb0.3 wd.2 ix.2 qb0.2 thn.1 wd.1 qb0.1
+qb0.6 qb0.4 b4.4 b3.3 cc.1 lf.5 tc.1 b6.7 b1.3 b2.3 tc.2 val.1 b0.2 qb0.5 b4.5 ab.1 tc.3 tb.3 tb.5 col.14 tc.4 b0.4 tb.1 b5.4
+b0.3 b1.5 tc.5 snd.1 tb.2 b1.4 b2.5 b6.8 tb.4 csb.2 yz.10 yz.11 b2.4 b0.5 yz.12 b5.5 b6.9 arr.1 ec.1 b7.3 b0.6 b6.10 b0.7
+eb.1 b5.6 b4.6 m1.1 hi.2 G8.1 yz.13 b0.8 b5.7 b5.8 yz.15 yz.14 b5.9 b5.10 mk.4 pw.1 E8.1 col.12 col.15 WM.1 lf.6 WM.3 yz.16
+cd.4 cs.5 b0.9 b6.11 b6.12 b6.13 cu.4 b4.7 ff.1 yz.2 b3.4 WM.4 t1.4 mw.2 wt.4 WM.2 lf.8 b1.6 du.4 ls.6 m1.2 b4.8 wi.1 tq.1
+b3.5 b5.11 ce.1 cc.2 m1.3 lf.7 lf.12 lf.11 wrd.2 b7.4 vt.3 b2.6 wrd.3 ls.3 yy.1 ix.3 ls.2 qb1.2 ix.4 qb1.1 tr.1 qb1.6 qb1.3
+val.2 tc.6 snd.2 qb1.4 ab.2 tb.6 qb1.5 b6.14 tb.8 b0.10 b4.9 tc.7 tc.9 b2.7 tb.7 csb.3 tc.8 b0.11 b1.7 b0.12 b6.15 b1.9 b5.12
+tb.9 b1.8 b7.5 b2.8 yz.17 tb.10 arr.2 m2.1 b6.17 b2.9 b0.13 b5.13 yz.18 b0.14 b6.16 tc.10 b0.16 b4.10 yz.19 eb.2 b5.14 b0.15
+ec.2 yz.20 b4.11 yz.22 b5.15 yz.6 yz.21 yz.4 b5.16 yz.5 b5.17 b5.18 mk.5 yz.23 cd.5 b3.6 yz.9 yz.7 cs.6 b6.18 b6.19 cu.5 tq.2
+b6.20 vt.4 t1.5 wt.5 du.5 b4.12 mw.3 m2.2 b3.7 yz.8 b4.13 ls.4 ls.7 ce.2 m2.3 b5.19 wrd.4 ff.2 b7.6 lf.10 cc.3 b6.21 wi.2
+wrd.5 ix.5 b2.10 b0.17 val.3 yy.2 qb2.1 qb2.2 tr.2 ix.6 qb2.3 b1.10 b5.20 qb2.6 b4.14 b1.11 qb2.5 qb2.4 snd.3 b6.22 b2.11
+tb.11 b0.18 tb.12 ab.3 tc.11 b0.20 b0.19 tc.12 b1.13 tc.14 b1.12 tc.13 b2.13 b6.24 yz.24 csb.4 tb.13 b2.12 tb.14 b7.7 arr.3
+m3.1 tc.15 b5.21 b6.23 yz.25 tb.15 b4.15 b0.21 b0.22 b0.23 yz.26 b0.24 b5.22 ec.3 eb.3 b4.16 b5.23 yz.27 yz.28 b5.24 yz.29
+b5.25 ff.3 b5.26 mk.6 cd.6 cs.7 b3.8 b6.25 yz.30 tq.3 cu.6 b6.26 b6.27 t1.6 wt.6 b4.17 du.6 m3.2 b3.9 mw.4 b4.18 wi.3 ls.8
+cc.4 m3.3 wrd.6 wrd.7 ce.3 cc.5 b5.27 ix.7 qb3.2 yy.3 b7.8 b4.19 qb3.3 b1.14 ix.8 qb3.1 b2.14 b6.28 tr.3 tc.16 qb3.6 ab.4
+tb.16 b4.20 b0.25 qb3.4 tc.17 b0.26 b1.15 b0.28 csb.5 qb3.5 b7.9 snd.4 f1.1 b7.10 arr.4 b0.27 b1.17 yz.31 b2.15 f2.1 b0.29
+tb.17 b1.16 ec.4 tb.18 eb.4 tb.20 fu.1 b4.21 yz.36 b2.16 yo.1 y.1 tc.19 yz.32 tc.18 tb.19 b6.29 yo.2 b2.17 yz.33 yo.3 tc.20
+y.2 b6.31 b6.30 yz.34 y.3 b0.30 b0.31 b0.32 yz.35 yo.4 yo.5 y.4 yo.7 yo.6 y.5
+"""
+CYCLE, PE_CYCLE, GATHER, SCATTER, WAKE, DMA_FIX, DMA_RATE, REMOTE, REMOTE_FIRST = 0.83e-3, 0.42e-3, 1.56, 3.5, 0.13, 1.3, 3.2e5, 2.0, 2.5
 BF, F32, I32, U16 = "bfloat16", "float32", "int32", "uint16"
 
 SCRATCH = {"ws": ("sbuf", [128, 12, 16], BF), "wd": ("sbuf", [128, 12, 128], BF)}
 for _dt, _bufs in (
-        (BF, dict(xs=S, vs=8, JH=144, JG=128, z=256, za=128, tab=256, hi=384, wt=384, vt=576, bcode=144, bcm=144, bcs=144,
-                  bd=152, dm=14 * 128, G=128, L0=128, L1=128, BI=128, cb=128, ones=512, mk0=200, cs0=200, mkf=136, csf=136,
-                  val=136, ab=576, csb=200, tb=CAP, tc=CAP, eb=64, ec=64)),
-        (F32, dict(yo=S, J=384, col=32, pw0=8, pw=8, rv=16, gm=8, nt=192, dt_=24, cv=132, tp=36, thf=4, thb=4, gf=4, gf2=4,
-                   vf=4, ta=24, tb_=24, cc=8, f1=192, f2=192)),
-        (I32, dict(thi=4, gpi=4, pi=4, pa=4)),
-        (U16, dict(lm=160, lp=160, cu=24, du=24, ix=128, fu=192))):
+        (BF, dict(xs=S, yz=ZO[-1] + CAP, vg=64, ET=144, vb=8, J=192, JG=128, z=128, zx=256, tab=256, hi0=640, hi=640, wt=384, vt=576,
+                  E=144, E8=144, G8=128, I8=128, LN=128, c44=192, pw=8, WM=512, mw=136, qq=192, ce=192, pat=128,
+                  pm=128, Sm=128, bd=152, dm=14 * 128, G=128, L0=128, L1=512, I=128, NI=128, DI=128, cb=128, ones=512,
+                  mk=256, cs=5 * 208, cd=256, val=128, ab=768, csb=200, tb=CAP, tc=CAP, eb=64, ec=64)),
+        (F32, dict(yo=S, col=32, rv=16, gm=8, nt=196, cv=128, thf=8, tf=8, GT=128, thb=4, thn=4, gn=4, gp=4, vf=4, t1=24, cc=8, f1=192,
+                   f2=192, ff=192, wrd=260, yy=192, tq=192, tr=192, lf=D * LW)),
+        (I32, dict(tg=8, pa=4)),
+        (U16, dict(ls=D * LW, cu=24, du=24, ix=132, fu=192, wi=12))):
     for _n, _w in _bufs.items():
         SCRATCH[_n] = ("sbuf", [128, _w], _dt)
 for _t in range(D):
-    SCRATCH["yz%d" % _t] = ("sbuf", [128, S + CAP + H], BF)
     SCRATCH["qb%d" % _t] = ("sbuf", [128, QW], BF)
-    SCRATCH["m%d" % _t] = ("sbuf", [128, 16 + DUMP + 384], BF)
+    SCRATCH["m%d" % _t] = ("sbuf", [128, MW], BF)
 for _b in range(8):
     SCRATCH["b%d" % _b] = ("psum", [128, 512], F32)
 
@@ -40,52 +76,74 @@ SEMAPHORES = ["sV", "sA", "sP", "sG", "sent", "ys"] + ["arr%d" % t for t in rang
 
 
 def build(g, core, T, topo, rank):
-    ops = []
+    ops, unit = [], [0, None, False]
     V, A, P = g.vector, g.scalar, g.tensor
 
-    def op(eng, fn, rd, wr, sem=None, val=None):
-        ops.append({"e": eng, "fn": fn, "rd": rd, "wr": wr, "sem": sem, "val": val})
+    def op(eng, fn, rd, wr, cost, sem=None, val=None, edge=None):
+        if unit[2]:
+            unit[2] = False
+        elif not (eng == "P" and ops and ops[-1]["e"] == "P"):
+            unit[0] += 1
+        ops.append({"e": eng, "fn": fn, "rd": [r[:3] for r in rd], "wr": [w[:3] for w in wr], "sem": sem, "val": val,
+                    "cost": cost, "unit": unit[0], "edge": edge, "step": unit[1], "name": None})
+
+    def cut():
+        unit[0] += 1
 
     def ap(n, a, b, step=1):
         return T[n][:, a:b:step] if step != 1 else T[n][:, a:b]
+
+    def size(x):
+        return len(range(*x[1:]))
+
+    def vcost(o, ins, lst):
+        if lst is not None:
+            return 0.05 + GATHER * size(o) * CYCLE
+        per = 0.5 if all(SCRATCH[x[0]][2] in (BF, U16) for x in [o] + ins) else 1.0
+        if len(ins) == 2 and all(SCRATCH[x[0]][0] == "sbuf" for x in ins):
+            per *= 2
+        return max(64, per * size(o)) * CYCLE + 0.02
 
     def sc(x):
         return (ap(x[0], x[1], x[1] + 1), [(x[0], x[1], x[1] + 1)]) if isinstance(x, tuple) else (x, [])
 
     def src(i, lst):
         if lst is None:
-            return ap(*i), [i[:3]]
-        return ap(*i).indirect(ap(*lst)), [i[:3], lst]
+            return ap(*i), [i]
+        return ap(*i).indirect(ap(*lst)), [i, lst]
 
     def ts(o, i, s1, o0, s2=None, o1=None, lst=None):
         a1, r1 = sc(s1)
         a2, r2 = sc(s2)
         x, r = src(i, lst)
         if o1 is None:
-            op("V", lambda: V.tensor_scalar(ap(*o), x, a1, None, o0), r + r1, [o])
+            op("V", lambda: V.tensor_scalar(ap(*o), x, a1, None, o0), r + r1, [o], vcost(o, [i], lst))
         else:
-            op("V", lambda: V.tensor_scalar(ap(*o), x, a1, a2, o0, o1), r + r1 + r2, [o])
+            op("V", lambda: V.tensor_scalar(ap(*o), x, a1, a2, o0, o1), r + r1 + r2, [o], vcost(o, [i], lst))
 
     def tt(o, i0, i1, o0, lst=None):
         x, r = src(i0, lst)
-        op("V", lambda: V.tensor_tensor(ap(*o), x, ap(*i1), o0), r + [i1], [o])
+        op("V", lambda: V.tensor_tensor(ap(*o), x, ap(*i1), o0), r + [i1], [o], vcost(o, [i0, i1], lst))
 
     def cp(o, i, lst=None):
         x, r = src(i, lst)
-        op("V", lambda: V.tensor_copy(ap(*o), x), r, [o])
+        op("V", lambda: V.tensor_copy(ap(*o), x), r, [o], vcost(o, [i], lst))
+
+    def scatter(win, lst, i):
+        op("V", lambda: V.tensor_copy(ap(*win).indirect(ap(*lst)), ap(*i)), [i, lst], [win], 0.05 + SCATTER * size(i) * CYCLE)
 
     def ms(o, c):
-        op("V", lambda: V.memset(ap(*o), c), [], [o])
+        op("V", lambda: V.memset(ap(*o), c), [], [o], vcost(o, [], None))
 
-    def scan(o, i, first=0.0, op0=ALU.add, op1=ALU.max):
-        a1, r1 = sc(first)
-        op("V", lambda: V.tensor_tensor_scan(ap(*o), ap(*i), ap(*i), a1, op0, op1), [i] + r1, [o])
+    def scan(o, i0, i1, op0, op1):
+        op("V", lambda: V.tensor_tensor_scan(ap(*o), ap(*i0), ap(*i1), 0.0, op0, op1), [i0, i1], [o], vcost(o, [i0], None))
 
-    def act(o, i, scale=1.0, bias=0.0, lst=None):
+    def act(o, i, scale=1.0, bias=0.0, lst=None, func=ACTF.Identity, more=0.0):
         a1, r1 = sc(scale)
         a2, r2 = sc(bias)
         x, r = src(i, lst)
-        op("A", lambda: A.activation(ap(*o), x, ACTF.Identity, bias=a2, scale=a1), r + r1 + r2, [o])
+        cost = 0.065 + GATHER * size(o) * CYCLE if lst else max(64, size(o)) * CYCLE + 0.04
+        op("A", lambda: A.activation(ap(*o), x, func, bias=a2, scale=a1), r + r1 + r2, [o], cost + more)
 
     def gat(eng, o, win, lst, scale=1.0, bias=0.0):
         if eng == "A":
@@ -95,115 +153,117 @@ def build(g, core, T, topo, rank):
         else:
             ts(o, win, scale, ALU.mult, bias, ALU.add, lst)
 
-    def mm(o, l, r, start, stop):
+    def rint(eng, o, i, tmp=None):
+        if eng == "A":
+            act((tmp, 0, size(o)), i, 1.0, ROUND)
+            unit[2] = True
+            act(o, (tmp, 0, size(o)), 1.0, -ROUND)
+        else:
+            ts(o, i, ROUND, ALU.add, ROUND, ALU.subtract)
+            ops[-1]["name"] = tmp
+
+    def mm(o, l, r, start, stop, group=None):
         lap = T.wd[:, l[1], :] if l[0] == "wd" else ap(*l)
         lr = ("wd", 0, 128) if l[0] == "wd" else l
-        op("P", lambda: P.matmul(ap(*o), lap, ap(*r), start, stop), [lr, r[:3]], [o])
+        e = {"start": start, "stop": stop, "group": group}
+        op("P", lambda: P.matmul(ap(*o), lap, ap(*r), start, e["stop"]), [lr, r], [o], max(64, size(o)) * PE_CYCLE, edge=e)
 
     def iota(o, pat, base=0, mult=0):
-        if o[0] == "pi":
-            op("G", lambda: g.iota(ap(*o), pat, base, mult), [], [o])
+        cost = 0.13 + 2 * size(o) * CYCLE
+        if o[0] == "pa":
+            op("G", lambda: g.iota(ap(*o), pat, base, mult), [], [o], cost)
         else:
-            op("G", lambda: g.iota(ap(*o), pat, base, mult, allow_small_or_imprecise_dtypes=True), [], [o])
+            op("G", lambda: g.iota(ap(*o), pat, base, mult, allow_small_or_imprecise_dtypes=True), [], [o], cost)
 
     def asel(o, i, cmp, fill):
-        op("G", lambda: g.affine_select(ap(*o), ap(*i), [[1, 128]], cmp, fill, 0, -1), [i], [o])
+        op("G", lambda: g.affine_select(ap(*o), ap(*i), [[1, 128]], cmp, fill, 0, -1), [i], [o], 0.17 + 256 * CYCLE)
 
     nd = [0]
 
-    def load(eng, o, dst, s):
+    def load(eng, o, dst, s, nbytes):
         q = g.sync if eng == "S" else A
-        op(eng, lambda: q.dma_start(dst, s), [], [o], "d%d" % nd[0], 16)
+        op(eng, lambda: q.dma_start(dst, s), [], [o], 0.1, "d%d" % nd[0], 16, edge=nbytes)
         nd[0] += 1
 
-    load("A", ("vs", 0, 4), T.vs[:, 0:4], T.v[:])
-    load("A", ("thi", 0, 4), T.thi[:], T.th[:])
-    for j in range(3):
-        load("S", ("xs", 1024 * j, 1024 * j + 1024), T.xs[:, 1024 * j:1024 * j + 1024], T.x[:, 1024 * j:1024 * j + 1024])
-    load("S", ("ws", 0, 16), T.ws[:], T.w[:])
-    load("S", ("gpi", 0, 4), T.gpi[:], T.gap[:])
+    def full(n, j=0):
+        return (n, 128 * j, 128 * j + 128)
 
-    G16, R, R8, HH, CA, CE, CD, WR, LO, TC_, HA, HB, CH, GG = range(14)
-    iota(("pi", 0, 1), [[0, 1]], 0, 1)
-    iota(("J", 0, 384), [[1, 384]])
-    iota(("JH", 0, 144), [[1, 72], [0, 2]])
-    iota(("JG", 0, 128), [[1, 8], [0, 16]])
-    iota(("m0", 0, DUMP), [[0, DUMP]])
-    iota(("ones", 0, 512), [[0, 512]], 1)
-    ms(("mk0", 192, 200), 0.0)
-    ms(("cs0", 0, 1), 0.0)
-    for j, bits in enumerate((112, 15, 7)):
-        ts(("pa", j, j + 1), ("pi", 0, 1), bits, ALU.bitwise_and)
-    cp(("col", 0, 3), ("pa", 0, 3))
+    def nt(a, b):
+        return ("nt", 2 + a, 2 + b)
 
-    def table():
-        ts(("z", 0, 1), ("col", R8, R8 + 1), 8.0, ALU.mult)
-        yield
-        for i in range(8):
-            n = 1 << i
-            ts(("za", 0, n), ("z", 0, n), -8.0, ALU.add, float(i - 8), ALU.max)
-            yield
-            tt(("z", n, 2 * n), ("z", 0, n), ("za", 0, n), ALU.min)
-            yield
-        ts(("tab", 0, 256), ("z", 0, 256), 0.0, ALU.min, ("col", TC_), ALU.max)
-        yield
+    def col(j):
+        return ("col", j, j + 1)
 
-    def c1(j, i, s1, o0, s2=None, o1=None):
-        ts(("col", j, j + 1), ("col", i, i + 1), s1, o0, s2, o1)
+    load("A", ("vg", 0, 64), T.vg[0:8, :], T.v[:], 1024)
+    load("S", ("tg", 0, 4), T.tg[0:8, 0:4], T.th[0:128:16, :], 128)
+    load("A", ("tg", 4, 8), T.tg[0:8, 4:8], T.gap[0:128:16, :], 128)
+    for a, b in zip(LOADS, LOADS[1:]):
+        load("S", ("xs", a, b), T.xs[:, a:b], T.x[:, a:b], 256 * (b - a))
+    load("S", ("ws", 0, 16), T.ws[:], T.w[:], 49152)
 
-    def c2(j, i, scale, bias):
-        act(("col", j, j + 1), ("col", i, i + 1), scale, bias)
-
-    def onehot(o, i, c, w=None):
-        if w is None:
-            ts(o, i, ("col", c), ALU.is_equal)
-        else:
-            ts(o, i, ("col", c), ALU.is_equal, w, ALU.mult)
-
-    def vtile(t):
-        onehot(("vt", 144 * t, 144 * t + 144), ("J", 0, 144), CE, ("vf", t))
-
-    def lists(t):
-        ts(("lm", 40 * t + 4, 40 * t + 36), ("tp", 0, 32), ("gf", t), ALU.subtract)
-        ts(("lp", 40 * t, 40 * t + 36), ("tp", 0, 36), ("gf", t), ALU.add)
-
-    def first_columns():
-        c1(HH, R, 8.0, ALU.is_ge)
-        for j, i, scale, bias in ((WR, HH, 7.0, 1.0), (GG, G16, 0.0625, 0.0), (LO, HH, -1.0, 1.0), (CH, G16, 0.5, 7.0),
-                                  (TC_, HH, 7.0, -8.0), (HA, HH, -1.0, 0.0), (HB, HH, 190.0, 1.0)):
-            c2(j, i, scale, bias)
-
-    early = [
-        first_columns,
-        lambda: c1(CE, G16, 15.0, ALU.add),
-        lambda: c1(CA, HH, ("col", G16), ALU.add, 14.0, ALU.add),
-        lambda: c1(CD, R8, ("col", CE), ALU.add),
-        lambda: ts(("pw0", 0, 8), ("J", 0, 8), ("col", R8), ALU.is_lt, 1.0, ALU.add),
-        lambda: ts(("rv", 0, 7), ("J", 1, 8), ("col", R8), ALU.is_le),
-        lambda: ts(("rv", 7, 14), ("J", 0, 7), ("col", R8), ALU.is_ge),
-        lambda: onehot(("bd", 0, 152), ("J", 0, 152), CD, ("col", WR)),
-        lambda: scan(("pw", 0, 8), ("pw0", 0, 8), -CB, ALU.mult, ALU.min),
-        lambda: onehot(("gm", 0, 8), ("J", 0, 8), GG),
-        lambda: cp(("vf", 0, 4), ("vs", 0, 4)),
-        lambda: onehot(("bcode", 0, 144), ("J", 0, 144), CA, ("pw", 7)),
-        lambda: vtile(0),
-        lambda: onehot(("bcm", 0, 144), ("J", 0, 144), CE, ("col", LO)),
-        lambda: onehot(("bcs", 0, 144), ("JH", 0, 144), CH),
-        lambda: cp(("thf", 0, 4), ("thi", 0, 4)),
-        lambda: onehot(("G", 0, 128), ("JG", 0, 128), GG),
-    ]
-    steps = table()
-    for j in range(18):
-        if j < len(early):
-            early[j]()
-        next(steps)
-    asel(("L0", 0, 128), ("G", 0, 128), ALU.is_gt, 0.0)
-    asel(("L1", 0, 128), ("L0", 0, 128), ALU.not_equal, float(S))
-    asel(("BI", 0, 128), ("L0", 0, 128), ALU.not_equal, BIG)
-    asel(("BI", 0, 128), ("BI", 0, 128), ALU.is_equal, 0.0)
-    act(("nt", 0, 192), ("J", 0, 192), 16.0, ("col", R))
-    act(("hi", 0, 384), ("J", 0, 384), ("col", HA), ("col", HB))
-    act(("dt_", 0, 24), ("nt", 0, 24), 1.0, float(DUMP))
+    R, H8, Q8, PP, G16, CD, LO, HH, TC_, DV, R15, PW, U1, U2, U3, U0, P16, RW = range(18)
+    iota(("pa", PP, PP + 1), [[0, 1]], 0, 1)
+    iota(("J", 0, 192), [[1, 192]])
+    iota(full("pat"), [[0, 16], [1, 8]])
+    iota(full("JG"), [[16, 8], [0, 16]])
+    ms(("ones", 0, 512), 1.0)
+    asel(full("I"), full("ones"), ALU.is_equal, 0.0)
+    for j, bits in ((R, 15), (H8, 8), (Q8, 56)):
+        ts(("pa", j, j + 1), ("pa", PP, PP + 1), bits, ALU.bitwise_and)
+    cp(("col", 0, 4), ("pa", 0, 4))
+    for j, i, scale, bias_ in ((G16, R, -1.0, ("col", PP)), (CD, H8, -1.0, ("col", PP)), (HH, H8, 0.125, 0.0), (LO, H8, -0.125, 1.0),
+                               (TC_, H8, 0.875, -8.0), (DV, R, 32.0, float(DUMP))):
+        act(col(j), col(i), scale, bias_)
+    for a in range(0, TAIL, TAIL // 4):
+        ms(("m0", a, a + TAIL // 4), 0.0)
+    ms(("cs", 0, 5 * 208, 208), 0.0)
+    ts(("rv", 0, 7), ("J", 1, 8), ("col", H8), ALU.add, ("col", R), ALU.is_le)
+    act(("rv", 7, 14), ("rv", 0, 7), -1.0, 1.0)
+    ts(("E", 0, 144), ("J", 0, 144), -15.0, ALU.add, ("col", G16), ALU.is_equal)
+    ts(("bd", 0, 152), ("J", 0, 152), -15.0, ALU.add, ("col", CD), ALU.is_equal)
+    ts(full("G"), full("JG"), ("col", G16), ALU.is_equal)
+    ts(full("Sm"), full("pat"), 8.0, ALU.mult, ("col", Q8), ALU.is_equal)
+    ts(full("pm"), full("pat"), 0.5, ALU.min)
+    act(col(P16), col(PP), 16.0)
+    ts(("ET", 0, 144), ("J", 0, 144), -15.0, ALU.add, ("col", P16), ALU.is_equal)
+    ts(full("GT"), full("JG"), ("col", P16), ALU.is_equal)
+    op("V", lambda: V.tensor_copy(T.tf[0:8, :], T.tg[0:8, :]), [("tg", 0, 8)], [("tf", 0, 8)], 0.08)
+    for c in range(16):
+        op("P", lambda c=c: P.matmul(T.b2[:, 0:4], T.ET[0:8, 15 - c:143 - c], T.vg[0:8, 4 * c:4 * c + 4], c == 0, c == 15),
+           [("ET", 0, 144), ("vg", 0, 64)], [("b2", 0, 4)], 64 * PE_CYCLE, edge={"start": c == 0, "stop": c == 15, "group": None})
+    cut()
+    op("P", lambda: P.matmul(T.b1[:, 0:8], T.GT[0:8, :], T.tf[0:8, :], True, True),
+       [full("GT"), ("tf", 0, 8)], [("b1", 0, 8)], 256 * PE_CYCLE, edge={"start": True, "stop": True, "group": None})
+    act(("vf", 0, 4), ("b2", 0, 4))
+    act(("thf", 0, 8), ("b1", 0, 8))
+    ts(("z", 0, 1), col(Q8), -0.125, ALU.mult, -0.5, ALU.add)
+    for i in range(7):
+        ts(("z", 1 << i, 2 << i), ("z", 0, 1 << i), ("rv", i - 1) if i else 1.0, ALU.add)
+    ts(("zx", 0, 128), full("z"), 0.0, ALU.is_lt)
+    ts(("zx", 128, 256), full("z"), ("rv", 6), ALU.add, 0.0, ALU.is_lt)
+    op("P", lambda: P.matmul(T.b3[:, 0:256], T.Sm[0:64, :], T.zx[0:64, :], True, True),
+       [full("Sm"), ("zx", 0, 256)], [("b3", 0, 256)], 256 * PE_CYCLE, edge={"start": True, "stop": True, "group": None})
+    ts(("tab", 0, 256), ("b3", 0, 256), -8.0, ALU.add, ("col", TC_), ALU.max)
+    for t in range(D):
+        act(("vt", 144 * t, 144 * t + 144), ("E", 0, 144), ("vf", t))
+    act(full("NI"), full("I"), -524288.0)
+    act(full("DI"), full("I"), ("col", DV))
+    for a, b, parts in ((0, 384, PARTS0), (384, 640, PARTS)):
+        for c0, w in parts:
+            iota(("hi0", a + c0 // 8, a + c0 // 8 + 2 * w), [[-8, w // 8], [-w, 16]], 1528 - c0)
+        if a:
+            act(("hi0", b - 49, b, 16), ("J", 0, 4), -8.0, 1560.0)
+        act(("hi", a, b), ("hi0", a, b), ("col", HH), ("col", LO))
+    asel(full("L0"), full("G"), ALU.is_gt, 0.0)
+    for t in range(D):
+        asel(full("L1", t), full("L0"), ALU.not_equal, float(ZO[t]))
+    for t in range(D):
+        for a in [0] * (rank == 0) + [QW - H] * (rank == len(T.cores) - 1):
+            unit[2] = True
+            iota(("qb%d" % t, a, a + H), [[0, H]])
+    asel(full("LN"), full("L0"), ALU.not_equal, -BIAS)
+    act(nt(0, 192), ("J", 0, 192), 16.0, ("col", R))
+    act(("nt", 0, 2), nt(0, 2), 1.0, float(CAP))
     diag = {}
     for dl in range(-7, 16):
         base = ("bd", 15 - dl, 143 - dl)
@@ -211,64 +271,54 @@ def build(g, core, T, topo, rank):
             diag[dl] = base
         else:
             j = -dl - 1 if dl < 0 else 22 - dl
-            diag[dl] = ("dm", 128 * j, 128 * j + 128)
+            diag[dl] = full("dm", j)
             act(diag[dl], base, ("rv", j))
+    act(full("cb"), full("ones"), BIAS / 128)
+    for t in range(D - 1):
+        iota(("yz", ZO[t] + MAIN, ZO[t] + CAP), [[0, H]])
+    iota(("csb", 0, 1), [[0, 1]])
+    iota(("mw", 128, 136), [[0, 8]], -1)
+    iota(("wrd", 256, 260), [[0, 4]])
+    k = 0
+    act(col(R15), col(R), 8192.0, -14.0 * 8192, func=ACTF.Relu)
+    for j, (c0, w) in enumerate(PARTS):
+        act(col(RW + j), col(R), -float(w), -float(c0 + H))
+        act(("cv", k, k + w), ("J", 0, w), -1.0, ("col", RW + j))
+        k += w
+    act(("cv", k - H, k), ("cv", k - H, k), 1.0, ("col", R15))
+    act(("gm", 0, 8), ("G", 0, 128, 16))
+    for q in range(8):
+        op("A", lambda q=q: A.activation(T.wd[:, :, 16 * q:16 * q + 16], T.ws[:], ACTF.Identity, scale=T.gm[:, q:q + 1]),
+           [("ws", 0, 16), ("gm", q, q + 1)], [("wd", 16 * q, 16 * q + 16)], 192 * CYCLE + 0.04)
+    act(("vb", 0, 4), ("vf", 0, 4), BIAS)
+    mm(("b3", 0, 4), full("G"), ("vb", 0, 4), True, True)
+    tt(("thb", 0, 4), ("b3", 0, 4), ("thf", 0, 4), ALU.add)
+    act(("thn", 0, 4), ("thb", 0, 4), -1.0, 0.5)
+    act(("gn", 0, 4), ("thf", 4, 8), -1.0, float(H))
+    act(("gp", 0, 4), ("thf", 4, 8), 1.0, float(H))
+    for t in range(D):
+        act(("lf", LW * t + 2, LW * t + 6), nt(0, 4))
+        act(("lf", LW * t + 6, LW * t + 38), nt(0, 32), 1.0, ("gn", t))
+        act(("lf", LW * t + 38, LW * t + 72), ("nt", 0, 34), 1.0, ("gp", t))
+        cp(("ls", LW * t + 6, LW * t + 72), ("lf", LW * t + 6, LW * t + 72))
+    act(("E8", 0, 144), ("E", 0, 144), 0.125)
+    act(full("G8"), full("G"), 0.125)
+    act(("c44", 0, 192), ("ones", 0, 192), -0.4375)
+    act(full("I8"), full("I"), -8.0)
+    act(("pw", 0, 1), col(R), math.log(2.0), func=ACTF.Exp, more=1.3)
+    act(col(U0), col(R), -1.0, 6.5, func=ACTF.Sign)
+    act(col(PW), ("pw", 0, 1))
+    act(col(U1), col(U0), 32768.0, 32768.0)
+    act(col(U2), col(H8), 1.0 / 2048)
+    act(col(U3), col(R15), -1.0 / 32, 256.0)
+    act(full("WM"), full("G"), ("col", PW))
+    for j, u in enumerate((U1, U2, U3)):
+        act(full("WM", j + 1), full("WM"), ("col", u))
+    for a in range(0, S, 512):
+        act(("yz", a, a + 512), ("xs", a, a + 512), 1.0, BIAS)
 
-    def weights():
-        for q in range(8):
-            op("A", lambda q=q: A.activation(T.wd[:, :, 16 * q:16 * q + 16], T.ws[:], ACTF.Identity, scale=T.gm[:, q:q + 1]),
-               [("ws", 0, 16), ("gm", q, q + 1)], [("wd", 16 * q, 16 * q + 16)])
-
-    def xcopy(n0=2048, n1=S):
-        act(("yz0", n0, n1), ("xs", n0, n1), 1.0, BIAS)
-
-    def later_a():
-        cp(("gf", 0, 4), ("gpi", 0, 4))
-        act(("cb", 0, 128), ("ones", 0, 128), BIAS / 128)
-        act(("gf2", 0, 4), ("gf", 0, 4), 1.0, float(S - H))
-
-    def later_b():
-        act(("tp", 0, 32), ("nt", 0, 32), 1.0, 32.0)
-        act(("tp", 32, 34), ("nt", 0, 2), 1.0, float(H + CAP))
-        act(("tp", 34, 36), ("nt", 0, 2), 1.0, 32.0)
-        act(("cv", 0, 126), ("nt", 0, 126), 1.0, float(S))
-        act(("cv", 126, 128), ("nt", 0, 2), 0.0, -1.0)
-        act(("cv", 128, 130), ("nt", 0, 2), 1.0, float(S))
-        for t in range(D):
-            if rank == 0:
-                iota(("qb%d" % t, 0, H), [[0, H]])
-            if rank == len(T.cores) - 1:
-                iota(("qb%d" % t, QW - H, QW), [[0, H]])
-        iota(("mkf", 128, 136), [[0, 8]])
-        iota(("csf", 0, 1), [[0, 1]])
-        iota(("csb", 0, 1), [[0, 1]])
-
-    def later_c():
-        mm(("b5", 0, 4), ("G", 0, 128), ("vs", 0, 4), True, True)
-        ts(("thb", 0, 4), ("b5", 0, 4), BIAS, ALU.mult, BIG, ALU.add)
-        vtile(1)
-        tt(("thb", 0, 4), ("thb", 0, 4), ("thf", 0, 4), ALU.add)
-
-    def yoff(t):
-        return H if t == D - 1 else 0
-
-    def zoff(t):
-        return S + yoff(t)
-
-    def scores(bank, t, buf, c0, k0, k1, alive):
-        o = (bank, k0, k1)
-        if alive is not None:
-            mm(o, ("BI", 0, 128), (alive[0], alive[1] + k0, alive[1] + k1), True, False)
-        for r in range(16):
-            mm(o, ("vt", 144 * t + 15 - r, 144 * t + 143 - r), (buf, c0 + 16 * k0 + r, c0 + 16 * k1, 16),
-               alive is None and r == 0, r == 15)
-
-    def merge(eng, t, n0, n1):
-        gat(eng, ("yz%d" % t, yoff(t) + n0, yoff(t) + n1), ("yz%d" % (t - 1), 0, S + CAP), ("fu", n0 // 16, n1 // 16))
-
-    def out(eng, n0, n1):
-        gat(eng, ("yo", n0, n1), ("yz%d" % (D - 1), 0, zoff(D - 1) + min(n1, MAIN)), ("fu", n0 // 16, n1 // 16), 1.0, -BIAS)
-        op("S", lambda: g.sync.dma_start(T.y[:, n0:n1], T.yo[:, n0:n1]), [("yo", n0, n1)], [], "ys", 16)
+    def vrow(t, r):
+        return ("vt", 144 * t + 15 - r, 144 * t + 143 - r)
 
     def send(t):
         qb = "qb%d" % t
@@ -286,192 +336,208 @@ def build(g, core, T, topo, rank):
             rid, pid = topo.addr(dst)[:2]
             tr.append(RemoteDMATransfer(dst_ids=[DstId(rid=rid, pnc=pid)], dma_engine_mask=sum(1 << x for x in e),
                                         remote_sem=T.sem["arr%d" % t], src=ap(*s), dst=ap(*d)))
-        op("G", lambda: g.remote_dma_fused(tr, local_sem=T.sem.sent), [p[1] for p in peers], [], "sent", NENG * len(peers))
-        op(None, None, [], [p[3] for p in peers], "arr%d" % t, NENG * len(peers))
+        op("G", lambda: g.remote_dma_fused(tr, local_sem=T.sem.sent), [(qb, H, 2 * H), (qb, H + CAP, 2 * H + CAP)], [], 0.1,
+           "sent", NENG * len(peers), edge="send")
+        op(None, None, [], [p[3] for p in peers], REMOTE + (REMOTE_FIRST if t == 0 else 0.0), "arr%d" % t, NENG * len(peers))
 
-    def keep(t, o, i):
-        ts(o, i, ("thf", 0) if t == 0 else ("thb", t), ALU.is_ge)
+    def bias(bank, n):
+        cut()
+        mm((bank, 0, n), full("cb"), ("ones", 0, n), True, False)
+        cut()
 
     for t in range(D):
-        K = (S if t == 0 else CAP) // 16
-        KU = K // 8
-        mk, cs = ("mk0", "cs0") if t == 0 else ("mkf", "csf")
-        qb, m, yz = "qb%d" % t, "m%d" % t, "yz%d" % t
-        lm, lp = 40 * t, 40 * t
-        cA, cB = ("cc", 2 * t), ("cc", 2 * t + 1)
+        qb, m, zo, lw = "qb%d" % t, "m%d" % t, ZO[t], LW * t
         last = t == D - 1
+        al, was = ("ab", 192 * t, 192 * t + 192), ("ab", 192 * t - 192, 192 * t)
+        th = ("thf", 0) if t == 0 else ("thb", t)
 
-        def step(w, k0, k1, bc, bp, mk=mk, cs=cs, m=m, K=K):
-            a, b = k0 // 8, k1 // 8
-            e = 8 if k1 == K else 0
-            if w == "c":
-                for q in range(8):
-                    mm((bc, a, b), ("bcode", 14 - 2 * q, 142 - 2 * q), (mk, k0 + q, k1, 8), q == 0, q == 7)
-            if w == "n":
-                scan((cs, k0 + 1, k1 + max(e, 1)), (mk, k0, k1 + max(e, 1) - 1), (cs, k0) if k0 else 0.0)
-            if w == "m":
-                o = (bp, a, (k1 + e) // 8)
-                for q in range(8):
-                    mm(o, ("bcm", 14 - 2 * q, 142 - 2 * q), (mk, k0 + q, k1 + e, 8), q == 0, False)
-                for q in range(8):
-                    mm(o, ("bcs", 14 - 2 * q, 142 - 2 * q), (cs, k0 + q, k1 + e, 8), False, q == 7)
-            if w == "u":
-                ts(("cu", a, b), (bc, a, b), -1.0 / CB, ALU.mult)
-            if w == "a":
-                tt(("ta", a, b), (bc, a, b), ("dt_", a, b), ALU.add)
-            if w == "w":
-                tt(("wt", 16 * a, 16 * b), ("tab", 0, 256), ("hi", 16 * a, 16 * b), ALU.mult, ("cu", a, b))
-            if w == "b":
-                tt(("tb_", a, b), (bp, a, b), ("ta", a, b), ALU.max)
-            if w == "d":
-                cp(("du", a, b), ("tb_", a, b))
-            if w == "p":
-                wn = (m, 16, 16 + DUMP + 384)
-                op("V", lambda: V.tensor_copy(ap(*wn).indirect(ap("du", a, b)), ap("wt", 16 * a, 16 * b)),
-                   [("wt", 16 * a, 16 * b), ("du", a, b)], [wn])
+        def on(name):
+            unit[1] = (t, name)
+            return "V" if name in ON_VECTOR[t] else "A"
 
-        if t == 0:
-            parts = [(0, 128, "b0", "b1"), (128, K, "b5", "b6")]
-            later_b()
-            xcopy(0, 2048)
-            weights()
-            for w in FRONT.split():
-                j = int(w[1])
-                if w[0] == "s":
-                    scores("b7" if j == 2 else "b4", 0, "xs", 0, 64 * j, 64 * j + 64, None)
-                elif w[0] == "k":
-                    keep(0, (mk,) + parts[j][:2], (("b4", "b7")[j],) + parts[j][:2])
-                else:
-                    step(w[0], *parts[j])
+        parts, k, ends = (PARTS0 if t == 0 else PARTS), 0, []
+        for j, (c0, w) in enumerate(parts):
+            sb, xb = (("b5", "b6"), ("b7", "b4"))[j % 2]
+            kc, a, nu = 208 * (j + (3 if t else 0)), k // 8, w // 8
+            b = a + nu
+            mk, codes = ("mk", k, k + w), ("cd", k + 7, k + w, 8)
+            on("list")
+            if t == 0:
+                for r in range(16):
+                    if c0 + w * r in LOADS:
+                        cut()
+                    mm((sb, 0, w), vrow(0, r), ("xs", c0 + w * r, c0 + w * r + w), r == 0, r == 15)
+            ts(mk, (sb, 0, w), th, ALU.is_ge)
+            scan(("cd", k, k + w), ("pm", 0, w), mk, ALU.mult, ALU.add)
+            scan(("cs", kc + 1, kc + w + 1), mk, mk, ALU.add, ALU.max)
+            mm((xb, 0, nu), full("I"), ("J", 0, nu), True, False)
+            mm((xb, 0, nu), full("DI"), ("ones", 0, nu), False, False)
+            cut()
+            mm((xb, 0, nu), full("NI"), codes, False, True)
+            cut()
+            ends.append(("cs", kc + w, kc + w + 1))
+            for c, own in ((32, "L0"), (33, "G"))[:2 if j == len(parts) - 1 else 1]:
+                for i, e in enumerate(ends):
+                    mm((xb, c, c + 1), full(own if i == j else "G"), e, i == 0, i == j)
+            ts(("cu", a, b), codes, 128.0, ALU.mult)
+            tt(("t1", a, b), (xb, 0, nu), ("cs", kc, kc + w, 8), ALU.max)
+            h = (384 if t else 0) + c0 // 8
+            tt(("wt", 16 * a, 16 * b), ("tab", 0, 256), ("hi", h, h + 2 * w), ALU.mult, ("cu", a, b))
+            ts(("du", a, b), ("t1", a, b), (xb, 32), ALU.add)
+            scatter((m, 16, MW), ("du", a, b), ("wt", 16 * a, 16 * b))
+            k += w
+        cnt = (xb, 33)
+        ts(("ls", lw, lw + 6), ("lf", lw + 2, lw + 8), cnt, ALU.add, float(-H), ALU.add)
+        if last:
+            act(("cc", 4, 5), cnt + (34,), 1.0, float(zo - H))
+            act(("cc", 5, 6), ("cc", 4, 5), -1.0, float(zo - H))
         else:
-            merge("A", t, 0, S - MERGE_V)
-            keep(t, (mk, 2, 66), ("b4", 2, 66))
-            lists(t)
-            if not last:
-                vtile(t + 1)
-            keep(t, (mk, 66, 128), ("b7", 66, 128))
-            keep(t, (mk, 0, 2), ("b7", 128, 130))
-            for w in "cnmuawbdp":
-                step(w, 0, K, "b5", "b6")
-                if w == "m":
-                    for j in range(3):
-                        mm(("b%d" % j, 0, CHUNKS[j][1]), ("cb", 0, 128), ("ones", 0, CHUNKS[j][1]), True, False)
-        for h, bank in enumerate(("b7", "b3")):
+            act(("cc", t, t + 1), cnt + (34,), -1.0, 1.0)
+            act(full("val"), full("cv"), -1.0, ("cc", t), func=ACTF.Relu)
+        gat(on("M"), (m, TAIL, TAIL + 48), (m, 0, TAIL - 16), ("ls", lw, lw + 3))
+        if t > 0:
+            on("T")
+            scatter(("yz", ZO[t - 1], ZO[t - 1] + CAP), ("ls", lw - LW, lw - LW + 2), ("yz", ZO[t - 1] - H, ZO[t - 1]))
+        on("D")
+        for h, (bank, n) in enumerate((("b5", 64), ("b7", 68))):
+            cut()
             for dl in range(-7, 16):
                 c0 = 16 + dl + 1024 * h
-                mm((bank, 0, 64), diag[dl], (m, c0, c0 + 1009, 16), dl == -7, dl == 15)
-        if t == 0:
-            later_a()
-            lists(0)
-        ts(cA + (cA[1] + 1,), ("b6", KU, KU + 1), float(S - H), ALU.add)
-        ts(cB + (cB[1] + 1,), ("b6", KU, KU + 1), -1.0, ALU.mult, float(-S if last else CAP), ALU.add)
-        ts(("lm", lm, lm + 2), ("nt", 0, 2), cA, ALU.add, float(-S), ALU.add)
-        ts(("lm", lm + 2, lm + 4), ("nt", 0, 2), cA, ALU.add, ("gf2", t), ALU.subtract)
-        if not last:
-            ts(("val", 0, 130), ("cv", 0, 130), cA, ALU.is_lt)
-        if t > 0 and MERGE_V:
-            merge("V", t, S - MERGE_V, S)
-        win = ("xs", 0, S) if t == 0 else ("yz%d" % (t - 1), S, S + CAP)
+                mm((bank, 0, n), diag[dl], (m, c0, c0 + 16 * n - 15, 16), dl == -7, dl == 15)
+            ts(("ix", 64 * h, 64 * h + n), (bank, 0, n), 1536.0 + (H if t else 0), ALU.add)
+        win = ("xs", 0, S) if t == 0 else ("yz", ZO[t - 1] - H, ZO[t - 1] + MAIN)
         qbias = 0.0 if t == 0 else -BIAS / 8
-
-        def qg(eng, c0, c1_):
-            gat(eng, (qb, H + c0, H + c1_), win, ("ix", c0 // 16, c1_ // 16), 0.125, qbias)
-
-        ts(("ix", 0, 64), ("b7", 0, 64), 1536.0, ALU.add)
-        qg("A", 0, 512)
-        qg("V", 512, 1024)
-        ts(("ix", 64, 128), ("b3", 0, 64), 1536.0, ALU.add)
-        qg("A", 1024, QSPLIT)
-        qg("V", QSPLIT, CAP)
-        gat("V", (qb, H + CAP, 2 * H + CAP), (qb, H, H + CAP), ("lm", lm, lm + 2))
+        for j, (c0, c1) in enumerate(zip(QCUT, QCUT[1:])):
+            gat(on("q%d" % j), (qb, H + c0, H + c1), win, ("ix", c0 // 16, c1 // 16), 0.125, qbias)
+        gat(on("tl"), (qb, H + CAP, 2 * H + CAP), win, ("ix", 130, 132), 0.125, qbias)
         send(t)
         if not last:
-            iota(("m%d" % (t + 1), 0, DUMP), [[0, DUMP]])
-        if t > 0:
-            al = ("ab", 192 * (t - 1))
-            scores("b5", t, yz, yoff(t), 0, 192, ("mk0", 0) if t == 1 else ("ab", 192 * (t - 2)))
+            iota(("m%d" % (t + 1), 0, TAIL), [[0, TAIL]])
+        on("X")
+        if t == 0:
+            for r in range(16):
+                mm(("b3", 64, 256), vrow(0, r), ("xs", r, S, 16), r == 0, r == 15)
+            ts(al, ("b3", 64, 256), th, ALU.is_ge)
         else:
-            al = ("mk0", 0)
-
-        def tap(eng, which, j):
-            c0, n = CHUNKS[j]
-            lst = ("lm", lm + 4, lm + 4 + n // 16) if which == "tb" else ("lp", lp, lp + n // 16)
-            gat(eng, (which, c0, c0 + n), (qb, c0, c0 + n + 2 * H), lst)
-
-        def head(j):
-            c0, n = CHUNKS[j]
-            o = ("b%d" % (j % 3), 0, n)
-            if j >= 3 or t == 0:
-                mm(o, ("cb", 0, 128), ("ones", 0, n), True, False)
-            mm(o, ("wd", 3 * t), (qb, H + c0, H + c0 + n), False, False)
-
-        def rest(j):
-            c0, n = CHUNKS[j]
-            o = ("b%d" % (j % 3), 0, n)
-            mm(o, ("wd", 3 * t + 1), ("tb", c0, c0 + n), False, False)
-            mm(o, ("wd", 3 * t + 2), ("tc", c0, c0 + n), False, True)
+            mm(("b3", 16, 208), full("I"), ("c44", 0, 192), True, False)
+            mm(("b3", 16, 208), full("G8"), ("csb", 0, 192), False, True)
+            mm(("b3", 0, 12), full("I"), ("c44", 0, 12), True, False)
+            for r in range(16):
+                mm(("b3", 0, 12), ("E8", 15 - r, 143 - r), ("csb", r, 192, 16), False, r == 15)
+            rint(on("Q"), ("qq", 0, 192), ("b3", 16, 208), "tq")
+            rint("V", ("wi", 0, 12), ("b3", 0, 12))
+            mm(("b3", 208, 400), full("LN"), was, True, False)
+            mm(("b3", 208, 400), full("G"), ("csb", 0, 192), False, False)
+            mm(("b3", 208, 400), full("I8"), ("qq", 0, 192), False, True)
+            act(("ce", 0, 192), ("b3", 208, 400), -math.log(2.0), -(BIAS + 2) * math.log(2.0), func=ACTF.Exp)
+            for r in range(16):
+                mm(("b4", 64, 192), vrow(t, r), ("yz", ZO[t - 1] + r, ZO[t - 1] + CAP, 16), r == 0, r == 15)
+            act(full("mw"), ("b4", 64, 192), 1.0, ("thn", t), func=ACTF.Sign)
+            for h in range(2):
+                o = ("b4", 192 + 128 * h, 320 + 128 * h)
+                mm(o, full("WM", 2 * h), full("mw"), True, False)
+                mm(o, full("WM", 2 * h + 1), ("mw", 1, 129), False, True)
+            for h in range(2):
+                gat(on("O%d" % h), ("wrd", h, 256, 2), ("b4", 192 + 128 * h, 320 + 128 * h), None, 1.0, 2.0 ** 23)
+            tt(("yy", 0, 192), ("wrd", 0, 258), ("ce", 0, 192), ALU.mult, ("wi", 0, 12))
+            rint(on("R"), ("b3", 0, 192), ("yy", 0, 192), "tr")
+            tt(al, ("b3", 0, 192), ("yy", 0, 192), ALU.is_gt)
+        on("F")
+        scan(("csb", 1, 193), al, al, ALU.add, ALU.max)
+        mm(("b7", 0, 192), full("L1", t), al, True, False)
+        mm(("b7", 0, 192), full("G"), ("csb", 0, 192), False, True)
+        if last:
+            ts(("f1", 0, 192), ("b7", 0, 192), ("cc", 4), ALU.is_ge, ("cc", 5), ALU.mult)
+            tt(("b7", 192, 384), ("b7", 0, 192), ("ff", 0, 192), ALU.max)
+            tt(("f2", 0, 192), ("b7", 192, 384), ("f1", 0, 192), ALU.add)
+            cp(("fu", 0, 192), ("f2", 0, 192))
+        else:
+            tt(("ff", 0, 192), ("b7", 0, 192), ("ff", 0, 192) if t else nt(0, 192), ALU.max)
 
         def clip(o, i):
             ts(o, i, BIAS - 15, ALU.max, BIAS + 15, ALU.min)
 
-        def evac(j):
-            c0, n = CHUNKS[j]
-            clip((yz, zoff(t) + c0, zoff(t) + c0 + n), ("b%d" % (j % 3), 0, n))
+        for j, (c0, n) in enumerate(CHUNKS):
+            o = (BANKS[j], 0, n)
+            gat(on("b%d" % j), ("tb", c0, c0 + n), (qb, c0, c0 + n + 2 * H), ("ls", lw + 6, lw + 6 + n // 16))
+            gat(on("c%d" % j), ("tc", c0, c0 + n), (qb, c0, c0 + n + 2 * H), ("ls", lw + 40, lw + 40 + n // 16))
+            on("e%d" % j)
+            bias(BANKS[j], n)
+            mm(o, ("wd", 3 * t), (qb, H + c0, H + c0 + n), False, False)
+            cut()
+            mm(o, ("wd", 3 * t + 1), ("tb", c0, c0 + n), False, False, (t, j))
+            cut()
+            mm(o, ("wd", 3 * t + 2), ("tc", c0, c0 + n), False, False, (t, j))
+            clip(("yz", zo + c0, zo + c0 + n), o)
+        gat(on("eb"), ("eb", 0, 64), (qb, 0, H + CAP), ("ls", lw + 4, lw + 8))
+        gat(on("ec"), ("ec", 0, 64), (qb, 0, QW), ("ls", lw + 38, lw + 42))
+        bias("b4", 64)
+        mm(("b4", 0, 32), ("wd", 3 * t), (qb, H + CAP, 2 * H + CAP), False, False)
+        mm(("b4", 32, 64), ("wd", 3 * t), (qb, H, 2 * H), False, False)
+        cut()
+        mm(("b4", 0, 64), ("wd", 3 * t + 1), ("eb", 0, 64), False, False)
+        mm(("b4", 0, 64), ("wd", 3 * t + 2), ("ec", 0, 64), False, True)
+        clip(("yz", zo - H, zo + H), ("b4", 0, 64))
+        if last:
+            for j, (n0, n1) in enumerate(zip(YCUT, YCUT[1:])):
+                gat(on("y%d" % j), ("yo", n0, n1), ("yz", 0, zo + min(n1, MAIN)), ("fu", n0 // 16, n1 // 16), 1.0, -BIAS)
+            for n0, n1 in zip(STORES, STORES[1:]):
+                op("S", lambda n0=n0, n1=n1: g.sync.dma_start(T.y[:, n0:n1], T.yo[:, n0:n1]), [("yo", n0, n1)], [], 0.1, "ys", 16,
+                   edge=512 * (n1 - n0))
+        else:
+            on("s")
+            w = PARTS[0][1]
+            mm(("b5", 0, w), full("NI"), full("val"), True, False)
+            for rows in ROWS:
+                cut()
+                for r in rows:
+                    n = w - H if r == 15 else w
+                    if n < w:
+                        mm(("b5", n, w), vrow(t + 1, r), ("yz", zo - H, zo), False, False, (t, "s"))
+                    mm(("b5", 0, n), vrow(t + 1, r), ("yz", zo + w * r, zo + w * r + n), False, False, (t, "s"))
+    return arrange(ops)
 
-        def fwd(j):
-            a = (al[0], al[1], al[1] + 192)
-            if j == 0 and t > 0:
-                keep(t, a, ("b5", 0, 192))
-            if j == 1:
-                if t > 0:
-                    scan(("csb", 1, 193), a)
-                mm(("b6", 0, 192), ("L1", 0, 128), a, True, False)
-                mm(("b6", 0, 192), ("G", 0, 128), ("cs0" if t == 0 else "csb", 0, 192), False, True)
-            if j == 2:
-                ts(("f1", 0, 192), ("b6", 0, 192), cA, ALU.is_ge, cB, ALU.mult)
-                tt(("b6", 192, 384), ("b6", 0, 192), ("nt", 0, 192), ALU.max)
-            if j == 3:
-                tt(("f2", 0, 192), ("b6", 192, 384), ("f1", 0, 192), ALU.add)
-            if j == 4:
-                ts(("fu", 0, 192), ("f2", 0, 192), float(yoff(t)), ALU.add)
 
-        def edge_g(eng):
-            gat(eng, ("eb", 0, 64), (qb, 0, H + CAP), ("lm", lm + 2, lm + 6))
-            gat(eng, ("ec", 0, 64), (qb, 0, QW), ("lp", lp + 32, lp + 36))
-
-        def edge_h():
-            mm(("b3", 0, 64), ("cb", 0, 128), ("ones", 0, 64), True, False)
-            mm(("b3", 0, 32), ("wd", 3 * t), (qb, H + CAP, 2 * H + CAP), False, False)
-            mm(("b3", 32, 64), ("wd", 3 * t), (qb, H, 2 * H), False, False)
-
-        def edge_r():
-            mm(("b3", 0, 64), ("wd", 3 * t + 1), ("eb", 0, 64), False, False)
-            mm(("b3", 0, 64), ("wd", 3 * t + 2), ("ec", 0, 64), False, True)
-
-        def edge_tail():
-            if last:
-                clip((yz, 0, H), ("b3", 0, 32))
-            else:
-                clip((yz, S + MAIN, S + CAP + H), ("b3", 0, 64))
-
-        def edge_head():
-            clip((yz, zoff(t), zoff(t) + H), ("b3", 32, 64))
-
-        for w in (LAST if last else FIRST if t == 0 else MID).split():
-            if w[1] in "bc" and w[0] in "AV":
-                tap(w[0], "t" + w[1], int(w[2]))
-            elif w[1] == "e":
-                edge_g(w[0])
-            elif w[1] == "y":
-                out(w[0], *(128 * int(x) for x in w[2:].split("-")))
-            elif w[0] in "href":
-                {"h": head, "r": rest, "e": evac, "f": fwd}[w[0]](int(w[1]))
-            elif w[0] == "s":
-                k0 = 2 + 64 * int(w[1])
-                scores("b7" if int(w[1]) else "b4", t + 1, yz, S, k0, k0 + 64, ("val", 0))
-            else:
-                {"gh": edge_h, "gr": edge_r, "gt": edge_tail, "gg": edge_head, "lc": later_c, "xc": xcopy}[w]()
-    return ops
+def arrange(ops):
+    units = {}
+    for i, o in enumerate(ops):
+        units.setdefault(o["unit"], []).append(i)
+    pred = {u: set() for u in units}
+    seen, prev = {}, {}
+    for i, o in enumerate(ops):
+        u = o["unit"]
+        acc = [(r, False) for r in o["rd"]] + [(r, True) for r in o["wr"]]
+        for (n, a, b), w in acc:
+            for j, a2, b2, w2 in seen.get(n, []):
+                p = ops[j]
+                if p["unit"] == u or not (w or w2):
+                    continue
+                if p["e"] == o["e"] == "P":
+                    if w and w2 and not (o["edge"]["group"] and o["edge"]["group"] == p["edge"]["group"]):
+                        pred[u].add(p["unit"])
+                elif a < b2 and a2 < b:
+                    pred[u].add(p["unit"])
+        for (n, a, b), w in acc:
+            seen.setdefault(n, []).append((i, a, b, w))
+        if o["e"] is None or (o["e"] == "G" and ops[i - 1]["e"] is None):
+            pred[u].add(ops[i - 1]["unit"])
+        if o["sem"] is not None and o["e"] in ("S", "A"):
+            if "dma" in prev:
+                pred[u].add(prev["dma"])
+            prev["dma"] = u
+    place, count = {}, {}
+    at = {n: i for i, n in enumerate(ORDER.split())}
+    for u, l in units.items():
+        o = ops[l[0]]
+        n = o["name"] or ("arr" if o["e"] is None else o["wr"][0][0] if o["wr"] else "snd" if o["e"] == "G" else "y")
+        count[n] = count.get(n, 0) + 1
+        place[u] = at["%s.%d" % (n, count[n])]
+    assert all(place[p] < place[u] for u in units for p in pred[u])
+    order = [ops[i] for u in sorted(units, key=place.get) for i in units[u]]
+    lastof = {o["edge"]["group"]: o for o in order if o["e"] == "P" and o["edge"]["group"]}
+    for o in lastof.values():
+        o["edge"]["stop"] = True
+    return order
 
 
 def emit(g, T, ops):

import math
from concourse.bass import DstId, RemoteDMATransfer
from concourse.mybir import AluOpType as ALU, ActivationFunctionType as ACTF

S, D, CAP, H = 3072, 4, 2048, 32
MAIN = CAP - H
ZO = [S + H + (CAP + H) * t for t in range(D)]
BIAS, ROUND = 192.0, 12582912.0
TAIL = 2080
DUMP = 2112
MW = 16 + DUMP + 512 + CAP
QW = CAP + 3 * H
LW = 72
CHUNKS = [(32, 480), (512, 512), (1024, 512), (1536, 384), (1920, 96)]
BANKS = ["b0", "b1", "b2", "b6", "b0"]
ROWS = [(1, 2, 3), (4, 5, 6, 7), (8, 9, 10, 11), (12, 13, 14), (0,), (15,)]
LOADS = [0, 1024, 2048, 3072]
PARTS0 = [(0, 64), (1024, 64), (2048, 64)]
PARTS = [(0, 128)]
QCUT = [0, 32, 544, 1024, 1568, 2048]
YCUT = [0, 512, 1024, 1536, 1920, 2304, 2688, 3072]
STORES = [0, 512, 1024, 1536, 2304, 3072]
NENG = 8
ON_VECTOR = [s.split() for s in ("M b0 b1 b3 ec q0 q2 q3 q4 tl", "O0 O1 Q R b2 c0 c1 c3 c4 q0 q1 tl", "O0 O1 Q R c0 c1 c3 q0 q2 q4",
                                 "O0 O1 R b4 c2 c4 eb q2 q3 q4 tl y1 y3 y6")]
PUSH = {}
ORDER = """
vg.1 tg.1 tg.2 pa.1 ones.1 cb.1 pa.3 pa.2 xs.1 pa.4 col.1 col.8 m0.1 z.1 col.2 pat.1 col.3 col.7 J.1 b0.1 I.1 JG.1 pm.1 col.4
nt.1 col.5 DI.1 ET.1 xs.2 b2.1 hi0.3 z.2 cs.1 rv.1 Sm.1 bd.1 z.3 m0.2 z.4 hi0.1 col.6 GT.1 rv.2 vf.1 dm.6 b2.2 b4.1 z.5 tf.1
E.1 hi0.2 col.10 yz.1 csb.1 dm.8 z.6 G.1 b1.1 L0.1 NI.1 vt.1 thf.1 z.7 c44.1 vb.1 b1.2 dm.10 b5.1 dm.12 dm.13 hi0.4 dm.4 m0.4
z.8 m0.3 zx.2 dm.1 hi.1 L1.2 dm.9 zx.1 b3.1 dm.7 dm.11 b7.1 gm.1 mk.1 cs.2 cd.1 yz.3 gp.1 tab.1 dm.3 b6.1 cu.1 mk.2 L1.1 b6.2
b6.3 t1.1 b3.2 cd.2 mw.1 wrd.1 nt.2 gn.1 cv.1 dm.2 LN.1 L1.3 b4.2 wt.1 cs.3 xs.3 du.1 dm.14 cu.2 b5.2 lf.2 b6.4 t1.2 m0.5
mk.3 b4.3 wt.2 lf.1 dm.5 cd.3 du.2 cs.4 col.11 ws.1 wd.3 wd.8 lf.3 b6.5 b6.6 wd.5 hi0.5 vt.2 col.9 wd.6 cu.3 m0.6 col.13 I8.1
wd.7 L1.4 t1.3 lf.4 lf.9 wt.3 du.3 m0.7 ls.5 b5.3 cv.2 wd.4 m0.8 b7.2 thb.1 ix.1 ls.1 qb0.3 wd.2 ix.2 qb0.2 thn.1 wd.1 qb0.1
qb0.6 qb0.4 b4.4 b3.3 cc.1 lf.5 tc.1 b6.7 b1.3 b2.3 tc.2 val.1 b0.2 qb0.5 b4.5 ab.1 tc.3 tb.3 tb.5 col.14 tc.4 b0.4 tb.1 b5.4
b0.3 b1.5 tc.5 snd.1 tb.2 b1.4 b2.5 b6.8 tb.4 csb.2 yz.10 yz.11 b2.4 b0.5 yz.12 b5.5 b6.9 arr.1 ec.1 b7.3 b0.6 b6.10 b0.7
eb.1 b5.6 b4.6 m1.1 hi.2 G8.1 yz.13 b0.8 b5.7 b5.8 yz.15 yz.14 b5.9 b5.10 mk.4 pw.1 E8.1 col.12 col.15 WM.1 lf.6 WM.3 yz.16
cd.4 cs.5 b0.9 b6.11 b6.12 b6.13 cu.4 b4.7 ff.1 yz.2 b3.4 WM.4 t1.4 mw.2 wt.4 WM.2 lf.8 b1.6 du.4 ls.6 m1.2 b4.8 wi.1 tq.1
b3.5 b5.11 ce.1 cc.2 m1.3 lf.7 lf.12 lf.11 wrd.2 b7.4 vt.3 b2.6 wrd.3 ls.3 yy.1 ix.3 ls.2 qb1.2 ix.4 qb1.1 tr.1 qb1.6 qb1.3
val.2 tc.6 snd.2 qb1.4 ab.2 tb.6 qb1.5 b6.14 tb.8 b0.10 b4.9 tc.7 tc.9 b2.7 tb.7 csb.3 tc.8 b0.11 b1.7 b0.12 b6.15 b1.9 b5.12
tb.9 b1.8 b7.5 b2.8 yz.17 tb.10 arr.2 m2.1 b6.17 b2.9 b0.13 b5.13 yz.18 b0.14 b6.16 tc.10 b0.16 b4.10 yz.19 eb.2 b5.14 b0.15
ec.2 yz.20 b4.11 yz.22 b5.15 yz.6 yz.21 yz.4 b5.16 yz.5 b5.17 b5.18 mk.5 yz.23 cd.5 b3.6 yz.9 yz.7 cs.6 b6.18 b6.19 cu.5 tq.2
b6.20 vt.4 t1.5 wt.5 du.5 b4.12 mw.3 m2.2 b3.7 yz.8 b4.13 ls.4 ls.7 ce.2 m2.3 b5.19 wrd.4 ff.2 b7.6 lf.10 cc.3 b6.21 wi.2
wrd.5 ix.5 b2.10 b0.17 val.3 yy.2 qb2.1 qb2.2 tr.2 ix.6 qb2.3 b1.10 b5.20 qb2.6 b4.14 b1.11 qb2.5 qb2.4 snd.3 b6.22 b2.11
tb.11 b0.18 tb.12 ab.3 tc.11 b0.20 b0.19 tc.12 b1.13 tc.14 b1.12 tc.13 b2.13 b6.24 yz.24 csb.4 tb.13 b2.12 tb.14 b7.7 arr.3
m3.1 tc.15 b5.21 b6.23 yz.25 tb.15 b4.15 b0.21 b0.22 b0.23 yz.26 b0.24 b5.22 ec.3 eb.3 b4.16 b5.23 yz.27 yz.28 b5.24 yz.29
b5.25 ff.3 b5.26 mk.6 cd.6 cs.7 b3.8 b6.25 yz.30 tq.3 cu.6 b6.26 b6.27 t1.6 wt.6 b4.17 du.6 m3.2 b3.9 mw.4 b4.18 wi.3 ls.8
cc.4 m3.3 wrd.6 wrd.7 ce.3 cc.5 b5.27 ix.7 qb3.2 yy.3 b7.8 b4.19 qb3.3 b1.14 ix.8 qb3.1 b2.14 b6.28 tr.3 tc.16 qb3.6 ab.4
tb.16 b4.20 b0.25 qb3.4 tc.17 b0.26 b1.15 b0.28 csb.5 qb3.5 b7.9 snd.4 f1.1 b7.10 arr.4 b0.27 b1.17 yz.31 b2.15 f2.1 b0.29
tb.17 b1.16 ec.4 tb.18 eb.4 tb.20 fu.1 b4.21 yz.36 b2.16 yo.1 y.1 tc.19 yz.32 tc.18 tb.19 b6.29 yo.2 b2.17 yz.33 yo.3 tc.20
y.2 b6.31 b6.30 yz.34 y.3 b0.30 b0.31 b0.32 yz.35 yo.4 yo.5 y.4 yo.7 yo.6 y.5
"""
CYCLE, PE_CYCLE, GATHER, SCATTER, WAKE, DMA_FIX, DMA_RATE, REMOTE, REMOTE_FIRST = 0.83e-3, 0.42e-3, 1.56, 3.5, 0.13, 1.3, 3.2e5, 2.0, 2.5
BF, F32, I32, U16 = "bfloat16", "float32", "int32", "uint16"

SCRATCH = {"ws": ("sbuf", [128, 12, 16], BF), "wd": ("sbuf", [128, 12, 128], BF)}
for _dt, _bufs in (
        (BF, dict(xs=S, yz=ZO[-1] + CAP, vg=64, ET=144, vb=8, J=192, JG=128, z=128, zx=256, tab=256, hi0=640, hi=640, wt=384, vt=576,
                  E=144, E8=144, G8=128, I8=128, LN=128, c44=192, pw=8, WM=512, mw=136, qq=192, ce=192, pat=128,
                  pm=128, Sm=128, bd=152, dm=14 * 128, G=128, L0=128, L1=512, I=128, NI=128, DI=128, cb=128, ones=512,
                  mk=256, cs=5 * 208, cd=256, val=128, ab=768, csb=200, tb=CAP, tc=CAP, eb=64, ec=64)),
        (F32, dict(yo=S, col=32, rv=16, gm=8, nt=196, cv=128, thf=8, tf=8, GT=128, thb=4, thn=4, gn=4, gp=4, vf=4, t1=24, cc=8, f1=192,
                   f2=192, ff=192, wrd=260, yy=192, tq=192, tr=192, lf=D * LW)),
        (I32, dict(tg=8, pa=4)),
        (U16, dict(ls=D * LW, cu=24, du=24, ix=132, fu=192, wi=12))):
    for _n, _w in _bufs.items():
        SCRATCH[_n] = ("sbuf", [128, _w], _dt)
for _t in range(D):
    SCRATCH["qb%d" % _t] = ("sbuf", [128, QW], BF)
    SCRATCH["m%d" % _t] = ("sbuf", [128, MW], BF)
for _b in range(8):
    SCRATCH["b%d" % _b] = ("psum", [128, 512], F32)

NDMA = 8
SEMAPHORES = ["sV", "sA", "sP", "sG", "sent", "ys"] + ["arr%d" % t for t in range(D)] + ["d%d" % i for i in range(NDMA)]


def build(g, core, T, topo, rank):
    ops, unit = [], [0, None, False]
    V, A, P = g.vector, g.scalar, g.tensor

    def op(eng, fn, rd, wr, cost, sem=None, val=None, edge=None):
        if unit[2]:
            unit[2] = False
        elif not (eng == "P" and ops and ops[-1]["e"] == "P"):
            unit[0] += 1
        ops.append({"e": eng, "fn": fn, "rd": [r[:3] for r in rd], "wr": [w[:3] for w in wr], "sem": sem, "val": val,
                    "cost": cost, "unit": unit[0], "edge": edge, "step": unit[1], "name": None})

    def cut():
        unit[0] += 1

    def ap(n, a, b, step=1):
        return T[n][:, a:b:step] if step != 1 else T[n][:, a:b]

    def size(x):
        return len(range(*x[1:]))

    def vcost(o, ins, lst):
        if lst is not None:
            return 0.05 + GATHER * size(o) * CYCLE
        per = 0.5 if all(SCRATCH[x[0]][2] in (BF, U16) for x in [o] + ins) else 1.0
        if len(ins) == 2 and all(SCRATCH[x[0]][0] == "sbuf" for x in ins):
            per *= 2
        return max(64, per * size(o)) * CYCLE + 0.02

    def sc(x):
        return (ap(x[0], x[1], x[1] + 1), [(x[0], x[1], x[1] + 1)]) if isinstance(x, tuple) else (x, [])

    def src(i, lst):
        if lst is None:
            return ap(*i), [i]
        return ap(*i).indirect(ap(*lst)), [i, lst]

    def ts(o, i, s1, o0, s2=None, o1=None, lst=None):
        a1, r1 = sc(s1)
        a2, r2 = sc(s2)
        x, r = src(i, lst)
        if o1 is None:
            op("V", lambda: V.tensor_scalar(ap(*o), x, a1, None, o0), r + r1, [o], vcost(o, [i], lst))
        else:
            op("V", lambda: V.tensor_scalar(ap(*o), x, a1, a2, o0, o1), r + r1 + r2, [o], vcost(o, [i], lst))

    def tt(o, i0, i1, o0, lst=None):
        x, r = src(i0, lst)
        op("V", lambda: V.tensor_tensor(ap(*o), x, ap(*i1), o0), r + [i1], [o], vcost(o, [i0, i1], lst))

    def cp(o, i, lst=None):
        x, r = src(i, lst)
        op("V", lambda: V.tensor_copy(ap(*o), x), r, [o], vcost(o, [i], lst))

    def scatter(win, lst, i):
        op("V", lambda: V.tensor_copy(ap(*win).indirect(ap(*lst)), ap(*i)), [i, lst], [win], 0.05 + SCATTER * size(i) * CYCLE)

    def ms(o, c):
        op("V", lambda: V.memset(ap(*o), c), [], [o], vcost(o, [], None))

    def scan(o, i0, i1, op0, op1):
        op("V", lambda: V.tensor_tensor_scan(ap(*o), ap(*i0), ap(*i1), 0.0, op0, op1), [i0, i1], [o], vcost(o, [i0], None))

    def act(o, i, scale=1.0, bias=0.0, lst=None, func=ACTF.Identity, more=0.0):
        a1, r1 = sc(scale)
        a2, r2 = sc(bias)
        x, r = src(i, lst)
        cost = 0.065 + GATHER * size(o) * CYCLE if lst else max(64, size(o)) * CYCLE + 0.04
        op("A", lambda: A.activation(ap(*o), x, func, bias=a2, scale=a1), r + r1 + r2, [o], cost + more)

    def gat(eng, o, win, lst, scale=1.0, bias=0.0):
        if eng == "A":
            act(o, win, scale, bias, lst)
        elif scale == 1.0 and bias == 0.0:
            cp(o, win, lst)
        else:
            ts(o, win, scale, ALU.mult, bias, ALU.add, lst)

    def rint(eng, o, i, tmp=None):
        if eng == "A":
            act((tmp, 0, size(o)), i, 1.0, ROUND)
            unit[2] = True
            act(o, (tmp, 0, size(o)), 1.0, -ROUND)
        else:
            ts(o, i, ROUND, ALU.add, ROUND, ALU.subtract)
            ops[-1]["name"] = tmp

    def mm(o, l, r, start, stop, group=None):
        lap = T.wd[:, l[1], :] if l[0] == "wd" else ap(*l)
        lr = ("wd", 0, 128) if l[0] == "wd" else l
        e = {"start": start, "stop": stop, "group": group}
        op("P", lambda: P.matmul(ap(*o), lap, ap(*r), start, e["stop"]), [lr, r], [o], max(64, size(o)) * PE_CYCLE, edge=e)

    def iota(o, pat, base=0, mult=0):
        cost = 0.13 + 2 * size(o) * CYCLE
        if o[0] == "pa":
            op("G", lambda: g.iota(ap(*o), pat, base, mult), [], [o], cost)
        else:
            op("G", lambda: g.iota(ap(*o), pat, base, mult, allow_small_or_imprecise_dtypes=True), [], [o], cost)

    def asel(o, i, cmp, fill):
        op("G", lambda: g.affine_select(ap(*o), ap(*i), [[1, 128]], cmp, fill, 0, -1), [i], [o], 0.17 + 256 * CYCLE)

    nd = [0]

    def load(eng, o, dst, s, nbytes):
        q = g.sync if eng == "S" else A
        op(eng, lambda: q.dma_start(dst, s), [], [o], 0.1, "d%d" % nd[0], 16, edge=nbytes)
        nd[0] += 1

    def full(n, j=0):
        return (n, 128 * j, 128 * j + 128)

    def nt(a, b):
        return ("nt", 2 + a, 2 + b)

    def col(j):
        return ("col", j, j + 1)

    load("A", ("vg", 0, 64), T.vg[0:8, :], T.v[:], 1024)
    load("S", ("tg", 0, 4), T.tg[0:8, 0:4], T.th[0:128:16, :], 128)
    load("A", ("tg", 4, 8), T.tg[0:8, 4:8], T.gap[0:128:16, :], 128)
    for a, b in zip(LOADS, LOADS[1:]):
        load("S", ("xs", a, b), T.xs[:, a:b], T.x[:, a:b], 256 * (b - a))
    load("S", ("ws", 0, 16), T.ws[:], T.w[:], 49152)

    R, H8, Q8, PP, G16, CD, LO, HH, TC_, DV, R15, PW, U1, U2, U3, U0, P16, RW = range(18)
    iota(("pa", PP, PP + 1), [[0, 1]], 0, 1)
    iota(("J", 0, 192), [[1, 192]])
    iota(full("pat"), [[0, 16], [1, 8]])
    iota(full("JG"), [[16, 8], [0, 16]])
    ms(("ones", 0, 512), 1.0)
    asel(full("I"), full("ones"), ALU.is_equal, 0.0)
    for j, bits in ((R, 15), (H8, 8), (Q8, 56)):
        ts(("pa", j, j + 1), ("pa", PP, PP + 1), bits, ALU.bitwise_and)
    cp(("col", 0, 4), ("pa", 0, 4))
    for j, i, scale, bias_ in ((G16, R, -1.0, ("col", PP)), (CD, H8, -1.0, ("col", PP)), (HH, H8, 0.125, 0.0), (LO, H8, -0.125, 1.0),
                               (TC_, H8, 0.875, -8.0), (DV, R, 32.0, float(DUMP))):
        act(col(j), col(i), scale, bias_)
    for a in range(0, TAIL, TAIL // 4):
        ms(("m0", a, a + TAIL // 4), 0.0)
    ms(("cs", 0, 5 * 208, 208), 0.0)
    ts(("rv", 0, 7), ("J", 1, 8), ("col", H8), ALU.add, ("col", R), ALU.is_le)
    act(("rv", 7, 14), ("rv", 0, 7), -1.0, 1.0)
    ts(("E", 0, 144), ("J", 0, 144), -15.0, ALU.add, ("col", G16), ALU.is_equal)
    ts(("bd", 0, 152), ("J", 0, 152), -15.0, ALU.add, ("col", CD), ALU.is_equal)
    ts(full("G"), full("JG"), ("col", G16), ALU.is_equal)
    ts(full("Sm"), full("pat"), 8.0, ALU.mult, ("col", Q8), ALU.is_equal)
    ts(full("pm"), full("pat"), 0.5, ALU.min)
    act(col(P16), col(PP), 16.0)
    ts(("ET", 0, 144), ("J", 0, 144), -15.0, ALU.add, ("col", P16), ALU.is_equal)
    ts(full("GT"), full("JG"), ("col", P16), ALU.is_equal)
    op("V", lambda: V.tensor_copy(T.tf[0:8, :], T.tg[0:8, :]), [("tg", 0, 8)], [("tf", 0, 8)], 0.08)
    for c in range(16):
        op("P", lambda c=c: P.matmul(T.b2[:, 0:4], T.ET[0:8, 15 - c:143 - c], T.vg[0:8, 4 * c:4 * c + 4], c == 0, c == 15),
           [("ET", 0, 144), ("vg", 0, 64)], [("b2", 0, 4)], 64 * PE_CYCLE, edge={"start": c == 0, "stop": c == 15, "group": None})
    cut()
    op("P", lambda: P.matmul(T.b1[:, 0:8], T.GT[0:8, :], T.tf[0:8, :], True, True),
       [full("GT"), ("tf", 0, 8)], [("b1", 0, 8)], 256 * PE_CYCLE, edge={"start": True, "stop": True, "group": None})
    act(("vf", 0, 4), ("b2", 0, 4))
    act(("thf", 0, 8), ("b1", 0, 8))
    ts(("z", 0, 1), col(Q8), -0.125, ALU.mult, -0.5, ALU.add)
    for i in range(7):
        ts(("z", 1 << i, 2 << i), ("z", 0, 1 << i), ("rv", i - 1) if i else 1.0, ALU.add)
    ts(("zx", 0, 128), full("z"), 0.0, ALU.is_lt)
    ts(("zx", 128, 256), full("z"), ("rv", 6), ALU.add, 0.0, ALU.is_lt)
    op("P", lambda: P.matmul(T.b3[:, 0:256], T.Sm[0:64, :], T.zx[0:64, :], True, True),
       [full("Sm"), ("zx", 0, 256)], [("b3", 0, 256)], 256 * PE_CYCLE, edge={"start": True, "stop": True, "group": None})
    ts(("tab", 0, 256), ("b3", 0, 256), -8.0, ALU.add, ("col", TC_), ALU.max)
    for t in range(D):
        act(("vt", 144 * t, 144 * t + 144), ("E", 0, 144), ("vf", t))
    act(full("NI"), full("I"), -524288.0)
    act(full("DI"), full("I"), ("col", DV))
    for a, b, parts in ((0, 384, PARTS0), (384, 640, PARTS)):
        for c0, w in parts:
            iota(("hi0", a + c0 // 8, a + c0 // 8 + 2 * w), [[-8, w // 8], [-w, 16]], 1528 - c0)
        if a:
            act(("hi0", b - 49, b, 16), ("J", 0, 4), -8.0, 1560.0)
        act(("hi", a, b), ("hi0", a, b), ("col", HH), ("col", LO))
    asel(full("L0"), full("G"), ALU.is_gt, 0.0)
    for t in range(D):
        asel(full("L1", t), full("L0"), ALU.not_equal, float(ZO[t]))
    for t in range(D):
        for a in [0] * (rank == 0) + [QW - H] * (rank == len(T.cores) - 1):
            unit[2] = True
            iota(("qb%d" % t, a, a + H), [[0, H]])
    asel(full("LN"), full("L0"), ALU.not_equal, -BIAS)
    act(nt(0, 192), ("J", 0, 192), 16.0, ("col", R))
    act(("nt", 0, 2), nt(0, 2), 1.0, float(CAP))
    diag = {}
    for dl in range(-7, 16):
        base = ("bd", 15 - dl, 143 - dl)
        if 0 <= dl <= 8:
            diag[dl] = base
        else:
            j = -dl - 1 if dl < 0 else 22 - dl
            diag[dl] = full("dm", j)
            act(diag[dl], base, ("rv", j))
    act(full("cb"), full("ones"), BIAS / 128)
    for t in range(D - 1):
        iota(("yz", ZO[t] + MAIN, ZO[t] + CAP), [[0, H]])
    iota(("csb", 0, 1), [[0, 1]])
    iota(("mw", 128, 136), [[0, 8]], -1)
    iota(("wrd", 256, 260), [[0, 4]])
    k = 0
    act(col(R15), col(R), 8192.0, -14.0 * 8192, func=ACTF.Relu)
    for j, (c0, w) in enumerate(PARTS):
        act(col(RW + j), col(R), -float(w), -float(c0 + H))
        act(("cv", k, k + w), ("J", 0, w), -1.0, ("col", RW + j))
        k += w
    act(("cv", k - H, k), ("cv", k - H, k), 1.0, ("col", R15))
    act(("gm", 0, 8), ("G", 0, 128, 16))
    for q in range(8):
        op("A", lambda q=q: A.activation(T.wd[:, :, 16 * q:16 * q + 16], T.ws[:], ACTF.Identity, scale=T.gm[:, q:q + 1]),
           [("ws", 0, 16), ("gm", q, q + 1)], [("wd", 16 * q, 16 * q + 16)], 192 * CYCLE + 0.04)
    act(("vb", 0, 4), ("vf", 0, 4), BIAS)
    mm(("b3", 0, 4), full("G"), ("vb", 0, 4), True, True)
    tt(("thb", 0, 4), ("b3", 0, 4), ("thf", 0, 4), ALU.add)
    act(("thn", 0, 4), ("thb", 0, 4), -1.0, 0.5)
    act(("gn", 0, 4), ("thf", 4, 8), -1.0, float(H))
    act(("gp", 0, 4), ("thf", 4, 8), 1.0, float(H))
    for t in range(D):
        act(("lf", LW * t + 2, LW * t + 6), nt(0, 4))
        act(("lf", LW * t + 6, LW * t + 38), nt(0, 32), 1.0, ("gn", t))
        act(("lf", LW * t + 38, LW * t + 72), ("nt", 0, 34), 1.0, ("gp", t))
        cp(("ls", LW * t + 6, LW * t + 72), ("lf", LW * t + 6, LW * t + 72))
    act(("E8", 0, 144), ("E", 0, 144), 0.125)
    act(full("G8"), full("G"), 0.125)
    act(("c44", 0, 192), ("ones", 0, 192), -0.4375)
    act(full("I8"), full("I"), -8.0)
    act(("pw", 0, 1), col(R), math.log(2.0), func=ACTF.Exp, more=1.3)
    act(col(U0), col(R), -1.0, 6.5, func=ACTF.Sign)
    act(col(PW), ("pw", 0, 1))
    act(col(U1), col(U0), 32768.0, 32768.0)
    act(col(U2), col(H8), 1.0 / 2048)
    act(col(U3), col(R15), -1.0 / 32, 256.0)
    act(full("WM"), full("G"), ("col", PW))
    for j, u in enumerate((U1, U2, U3)):
        act(full("WM", j + 1), full("WM"), ("col", u))
    for a in range(0, S, 512):
        act(("yz", a, a + 512), ("xs", a, a + 512), 1.0, BIAS)

    def vrow(t, r):
        return ("vt", 144 * t + 15 - r, 144 * t + 143 - r)

    def send(t):
        qb = "qb%d" % t
        left, right = (qb, 0, H), (qb, QW - H, QW)
        peers = []
        if rank > 0:
            peers.append((T.cores[rank - 1], (qb, H, 2 * H), right, left))
        if rank < len(T.cores) - 1:
            peers.append((T.cores[rank + 1], (qb, H + CAP, 2 * H + CAP), left, right))
        peers.sort(key=lambda p: len(topo.engines(core, p[0])))
        used, tr = [], []
        for dst, s, d, _ in peers:
            e = [x for x in topo.engines(core, dst) if x not in used][:NENG]
            used += e
            rid, pid = topo.addr(dst)[:2]
            tr.append(RemoteDMATransfer(dst_ids=[DstId(rid=rid, pnc=pid)], dma_engine_mask=sum(1 << x for x in e),
                                        remote_sem=T.sem["arr%d" % t], src=ap(*s), dst=ap(*d)))
        op("G", lambda: g.remote_dma_fused(tr, local_sem=T.sem.sent), [(qb, H, 2 * H), (qb, H + CAP, 2 * H + CAP)], [], 0.1,
           "sent", NENG * len(peers), edge="send")
        op(None, None, [], [p[3] for p in peers], REMOTE + (REMOTE_FIRST if t == 0 else 0.0), "arr%d" % t, NENG * len(peers))

    def bias(bank, n):
        cut()
        mm((bank, 0, n), full("cb"), ("ones", 0, n), True, False)
        cut()

    for t in range(D):
        qb, m, zo, lw = "qb%d" % t, "m%d" % t, ZO[t], LW * t
        last = t == D - 1
        al, was = ("ab", 192 * t, 192 * t + 192), ("ab", 192 * t - 192, 192 * t)
        th = ("thf", 0) if t == 0 else ("thb", t)

        def on(name):
            unit[1] = (t, name)
            return "V" if name in ON_VECTOR[t] else "A"

        parts, k, ends = (PARTS0 if t == 0 else PARTS), 0, []
        for j, (c0, w) in enumerate(parts):
            sb, xb = (("b5", "b6"), ("b7", "b4"))[j % 2]
            kc, a, nu = 208 * (j + (3 if t else 0)), k // 8, w // 8
            b = a + nu
            mk, codes = ("mk", k, k + w), ("cd", k + 7, k + w, 8)
            on("list")
            if t == 0:
                for r in range(16):
                    if c0 + w * r in LOADS:
                        cut()
                    mm((sb, 0, w), vrow(0, r), ("xs", c0 + w * r, c0 + w * r + w), r == 0, r == 15)
            ts(mk, (sb, 0, w), th, ALU.is_ge)
            scan(("cd", k, k + w), ("pm", 0, w), mk, ALU.mult, ALU.add)
            scan(("cs", kc + 1, kc + w + 1), mk, mk, ALU.add, ALU.max)
            mm((xb, 0, nu), full("I"), ("J", 0, nu), True, False)
            mm((xb, 0, nu), full("DI"), ("ones", 0, nu), False, False)
            cut()
            mm((xb, 0, nu), full("NI"), codes, False, True)
            cut()
            ends.append(("cs", kc + w, kc + w + 1))
            for c, own in ((32, "L0"), (33, "G"))[:2 if j == len(parts) - 1 else 1]:
                for i, e in enumerate(ends):
                    mm((xb, c, c + 1), full(own if i == j else "G"), e, i == 0, i == j)
            ts(("cu", a, b), codes, 128.0, ALU.mult)
            tt(("t1", a, b), (xb, 0, nu), ("cs", kc, kc + w, 8), ALU.max)
            h = (384 if t else 0) + c0 // 8
            tt(("wt", 16 * a, 16 * b), ("tab", 0, 256), ("hi", h, h + 2 * w), ALU.mult, ("cu", a, b))
            ts(("du", a, b), ("t1", a, b), (xb, 32), ALU.add)
            scatter((m, 16, MW), ("du", a, b), ("wt", 16 * a, 16 * b))
            k += w
        cnt = (xb, 33)
        ts(("ls", lw, lw + 6), ("lf", lw + 2, lw + 8), cnt, ALU.add, float(-H), ALU.add)
        if last:
            act(("cc", 4, 5), cnt + (34,), 1.0, float(zo - H))
            act(("cc", 5, 6), ("cc", 4, 5), -1.0, float(zo - H))
        else:
            act(("cc", t, t + 1), cnt + (34,), -1.0, 1.0)
            act(full("val"), full("cv"), -1.0, ("cc", t), func=ACTF.Relu)
        gat(on("M"), (m, TAIL, TAIL + 48), (m, 0, TAIL - 16), ("ls", lw, lw + 3))
        if t > 0:
            on("T")
            scatter(("yz", ZO[t - 1], ZO[t - 1] + CAP), ("ls", lw - LW, lw - LW + 2), ("yz", ZO[t - 1] - H, ZO[t - 1]))
        on("D")
        for h, (bank, n) in enumerate((("b5", 64), ("b7", 68))):
            cut()
            for dl in range(-7, 16):
                c0 = 16 + dl + 1024 * h
                mm((bank, 0, n), diag[dl], (m, c0, c0 + 16 * n - 15, 16), dl == -7, dl == 15)
            ts(("ix", 64 * h, 64 * h + n), (bank, 0, n), 1536.0 + (H if t else 0), ALU.add)
        win = ("xs", 0, S) if t == 0 else ("yz", ZO[t - 1] - H, ZO[t - 1] + MAIN)
        qbias = 0.0 if t == 0 else -BIAS / 8
        for j, (c0, c1) in enumerate(zip(QCUT, QCUT[1:])):
            gat(on("q%d" % j), (qb, H + c0, H + c1), win, ("ix", c0 // 16, c1 // 16), 0.125, qbias)
        gat(on("tl"), (qb, H + CAP, 2 * H + CAP), win, ("ix", 130, 132), 0.125, qbias)
        send(t)
        if not last:
            iota(("m%d" % (t + 1), 0, TAIL), [[0, TAIL]])
        on("X")
        if t == 0:
            for r in range(16):
                mm(("b3", 64, 256), vrow(0, r), ("xs", r, S, 16), r == 0, r == 15)
            ts(al, ("b3", 64, 256), th, ALU.is_ge)
        else:
            mm(("b3", 16, 208), full("I"), ("c44", 0, 192), True, False)
            mm(("b3", 16, 208), full("G8"), ("csb", 0, 192), False, True)
            mm(("b3", 0, 12), full("I"), ("c44", 0, 12), True, False)
            for r in range(16):
                mm(("b3", 0, 12), ("E8", 15 - r, 143 - r), ("csb", r, 192, 16), False, r == 15)
            rint(on("Q"), ("qq", 0, 192), ("b3", 16, 208), "tq")
            rint("V", ("wi", 0, 12), ("b3", 0, 12))
            mm(("b3", 208, 400), full("LN"), was, True, False)
            mm(("b3", 208, 400), full("G"), ("csb", 0, 192), False, False)
            mm(("b3", 208, 400), full("I8"), ("qq", 0, 192), False, True)
            act(("ce", 0, 192), ("b3", 208, 400), -math.log(2.0), -(BIAS + 2) * math.log(2.0), func=ACTF.Exp)
            for r in range(16):
                mm(("b4", 64, 192), vrow(t, r), ("yz", ZO[t - 1] + r, ZO[t - 1] + CAP, 16), r == 0, r == 15)
            act(full("mw"), ("b4", 64, 192), 1.0, ("thn", t), func=ACTF.Sign)
            for h in range(2):
                o = ("b4", 192 + 128 * h, 320 + 128 * h)
                mm(o, full("WM", 2 * h), full("mw"), True, False)
                mm(o, full("WM", 2 * h + 1), ("mw", 1, 129), False, True)
            for h in range(2):
                gat(on("O%d" % h), ("wrd", h, 256, 2), ("b4", 192 + 128 * h, 320 + 128 * h), None, 1.0, 2.0 ** 23)
            tt(("yy", 0, 192), ("wrd", 0, 258), ("ce", 0, 192), ALU.mult, ("wi", 0, 12))
            rint(on("R"), ("b3", 0, 192), ("yy", 0, 192), "tr")
            tt(al, ("b3", 0, 192), ("yy", 0, 192), ALU.is_gt)
        on("F")
        scan(("csb", 1, 193), al, al, ALU.add, ALU.max)
        mm(("b7", 0, 192), full("L1", t), al, True, False)
        mm(("b7", 0, 192), full("G"), ("csb", 0, 192), False, True)
        if last:
            ts(("f1", 0, 192), ("b7", 0, 192), ("cc", 4), ALU.is_ge, ("cc", 5), ALU.mult)
            tt(("b7", 192, 384), ("b7", 0, 192), ("ff", 0, 192), ALU.max)
            tt(("f2", 0, 192), ("b7", 192, 384), ("f1", 0, 192), ALU.add)
            cp(("fu", 0, 192), ("f2", 0, 192))
        else:
            tt(("ff", 0, 192), ("b7", 0, 192), ("ff", 0, 192) if t else nt(0, 192), ALU.max)

        def clip(o, i):
            ts(o, i, BIAS - 15, ALU.max, BIAS + 15, ALU.min)

        for j, (c0, n) in enumerate(CHUNKS):
            o = (BANKS[j], 0, n)
            gat(on("b%d" % j), ("tb", c0, c0 + n), (qb, c0, c0 + n + 2 * H), ("ls", lw + 6, lw + 6 + n // 16))
            gat(on("c%d" % j), ("tc", c0, c0 + n), (qb, c0, c0 + n + 2 * H), ("ls", lw + 40, lw + 40 + n // 16))
            on("e%d" % j)
            bias(BANKS[j], n)
            mm(o, ("wd", 3 * t), (qb, H + c0, H + c0 + n), False, False)
            cut()
            mm(o, ("wd", 3 * t + 1), ("tb", c0, c0 + n), False, False, (t, j))
            cut()
            mm(o, ("wd", 3 * t + 2), ("tc", c0, c0 + n), False, False, (t, j))
            clip(("yz", zo + c0, zo + c0 + n), o)
        gat(on("eb"), ("eb", 0, 64), (qb, 0, H + CAP), ("ls", lw + 4, lw + 8))
        gat(on("ec"), ("ec", 0, 64), (qb, 0, QW), ("ls", lw + 38, lw + 42))
        bias("b4", 64)
        mm(("b4", 0, 32), ("wd", 3 * t), (qb, H + CAP, 2 * H + CAP), False, False)
        mm(("b4", 32, 64), ("wd", 3 * t), (qb, H, 2 * H), False, False)
        cut()
        mm(("b4", 0, 64), ("wd", 3 * t + 1), ("eb", 0, 64), False, False)
        mm(("b4", 0, 64), ("wd", 3 * t + 2), ("ec", 0, 64), False, True)
        clip(("yz", zo - H, zo + H), ("b4", 0, 64))
        if last:
            for j, (n0, n1) in enumerate(zip(YCUT, YCUT[1:])):
                gat(on("y%d" % j), ("yo", n0, n1), ("yz", 0, zo + min(n1, MAIN)), ("fu", n0 // 16, n1 // 16), 1.0, -BIAS)
            for n0, n1 in zip(STORES, STORES[1:]):
                op("S", lambda n0=n0, n1=n1: g.sync.dma_start(T.y[:, n0:n1], T.yo[:, n0:n1]), [("yo", n0, n1)], [], 0.1, "ys", 16,
                   edge=512 * (n1 - n0))
        else:
            on("s")
            w = PARTS[0][1]
            mm(("b5", 0, w), full("NI"), full("val"), True, False)
            for rows in ROWS:
                cut()
                for r in rows:
                    n = w - H if r == 15 else w
                    if n < w:
                        mm(("b5", n, w), vrow(t + 1, r), ("yz", zo - H, zo), False, False, (t, "s"))
                    mm(("b5", 0, n), vrow(t + 1, r), ("yz", zo + w * r, zo + w * r + n), False, False, (t, "s"))
    return arrange(ops)


def arrange(ops):
    units = {}
    for i, o in enumerate(ops):
        units.setdefault(o["unit"], []).append(i)
    pred = {u: set() for u in units}
    seen, prev = {}, {}
    for i, o in enumerate(ops):
        u = o["unit"]
        acc = [(r, False) for r in o["rd"]] + [(r, True) for r in o["wr"]]
        for (n, a, b), w in acc:
            for j, a2, b2, w2 in seen.get(n, []):
                p = ops[j]
                if p["unit"] == u or not (w or w2):
                    continue
                if p["e"] == o["e"] == "P":
                    if w and w2 and not (o["edge"]["group"] and o["edge"]["group"] == p["edge"]["group"]):
                        pred[u].add(p["unit"])
                elif a < b2 and a2 < b:
                    pred[u].add(p["unit"])
        for (n, a, b), w in acc:
            seen.setdefault(n, []).append((i, a, b, w))
        if o["e"] is None or (o["e"] == "G" and ops[i - 1]["e"] is None):
            pred[u].add(ops[i - 1]["unit"])
        if o["sem"] is not None and o["e"] in ("S", "A"):
            if "dma" in prev:
                pred[u].add(prev["dma"])
            prev["dma"] = u
    place, count = {}, {}
    at = {n: i for i, n in enumerate(ORDER.split())}
    for u, l in units.items():
        o = ops[l[0]]
        n = o["name"] or ("arr" if o["e"] is None else o["wr"][0][0] if o["wr"] else "snd" if o["e"] == "G" else "y")
        count[n] = count.get(n, 0) + 1
        place[u] = at["%s.%d" % (n, count[n])]
    assert all(place[p] < place[u] for u in units for p in pred[u])
    order = [ops[i] for u in sorted(units, key=place.get) for i in units[u]]
    lastof = {o["edge"]["group"]: o for o in order if o["e"] == "P" and o["edge"]["group"]}
    for o in lastof.values():
        o["edge"]["stop"] = True
    return order


def emit(g, T, ops):
    queue = {"V": g.vector, "A": g.scalar, "P": g.tensor, "G": g, "S": g.sync}
    seen = {}
    for i, o in enumerate(ops):
        dep = set()
        acc = [(r, False) for r in o["rd"]] + [(r, True) for r in o["wr"]]
        for (n, a, b), w in acc:
            psum = SCRATCH[n][0] == "psum"
            for j, a2, b2, w2 in seen.get(n, []):
                e2 = ops[j]["e"]
                if e2 == o["e"] == "P":
                    continue
                if (psum and e2 != o["e"]) or ((w or w2) and a < b2 and a2 < b):
                    dep.add(j)
        for (n, a, b), w in acc:
            seen.setdefault(n, []).append((i, a, b, w))
        lastof = {}
        for j in dep:
            k = ops[j]["e"] if ops[j]["sem"] is None else ("x", j)
            lastof[k] = max(lastof.get(k, -1), j)
        o["dep"] = sorted(lastof.values())
    known = {e: {} for e in queue}
    for i, o in enumerate(ops):
        if o["e"] is None:
            o["clock"], o["wait"] = {}, []
            continue
        kn = known[o["e"]]
        wait = []
        for j in sorted(o["dep"], reverse=True):
            p = ops[j]
            k = p["e"] if p["sem"] is None else ("x", j)
            if kn.get(k, -1) >= j:
                continue
            wait.append(j)
            kn[k] = j
            for k2, v in p["clock"].items():
                kn[k2] = max(kn.get(k2, -1), v)
        o["wait"] = wait
        o["clock"] = dict(kn)
    needed = set(j for o in ops for j in o["wait"])
    count = {}
    for i, o in enumerate(ops):
        if o["sem"] is None and i in needed:
            o["sem"], o["val"] = "s" + o["e"], 1
        if o["sem"] is not None:
            count[o["sem"]] = count.get(o["sem"], 0) + o["val"]
            o["at"] = count[o["sem"]]
    waited = {}
    for o in ops:
        if o["e"] is None:
            continue
        for j in o["wait"]:
            queue[o["e"]].wait_ge(T.sem[ops[j]["sem"]], ops[j]["at"])
            waited[ops[j]["sem"]] = max(waited.get(ops[j]["sem"], 0), ops[j]["at"])
        ins = o["fn"]()
        if o["sem"] is not None and o["sem"] != "sent":
            ins.then_inc(T.sem[o["sem"]], o["val"])
    for s, n in count.items():
        if waited.get(s, 0) < n:
            (g.sync if s == "ys" else g).wait_ge(T.sem[s], n)


def rank_program(g, core, T, topo):
    rank = T.rank_of(core)
    if rank is None:
        return
    emit(g, T, build(g, core, T, topo, rank))
